import numpy as np
import ml_dtypes


def mxq(x, axis, fmt="e4m3"):
    dtype, down = {"e4m3": (ml_dtypes.float8_e4m3fn, 7), "e5m2": (ml_dtypes.float8_e5m2, 14)}[fmt]
    v = np.moveaxis(np.asarray(x, np.float32).astype(ml_dtypes.bfloat16).astype(np.float64), axis, -1)
    blocks = v.reshape(v.shape[:-1] + (-1, 32))
    amax = np.abs(blocks).max(-1, keepdims=True)
    byte = np.maximum(np.where(amax > 0, np.frexp(amax)[1] - 1 + 127, 0) - down, 1)
    scale = np.exp2(byte - 127.0)
    codes = (blocks / scale).astype(np.float32).astype(dtype).astype(np.float64)
    return np.moveaxis((codes * scale).reshape(v.shape), -1, axis)


WIDE = False


def mx_kscale(k):
    if not WIDE:
        return np.ones(k)
    levels = np.array([10, -10, 5, -5, 0])
    if k % 512:
        return np.exp2(np.random.permutation(np.resize(levels, k // 32))).repeat(32)
    a = np.empty((k // 512, 16))
    for p in range(k // 512):
        a[p, :8] = np.random.permutation(np.resize(levels, 8))
        for g in range(8):
            far = levels[np.abs(levels - a[p, g]) >= 10]
            a[p, g + 8] = far[np.random.randint(len(far))]
    return np.exp2(a.ravel()).repeat(32)


def f64(x):
    return np.asarray(x).astype(np.float64)


def striped8(idx):
    return np.concatenate([x.reshape(-1, 16).T for x in idx]).astype(np.uint16)


def runs(offs, k):
    lists = np.stack([offs[16 * r : 16 * r + 16].T.reshape(-1) for r in range(8)]).astype(np.int64)
    return lists[np.arange(k) % 512 // 64]


def pack_weight(w):
    k, n = w.shape
    w = f64(np.asarray(w, np.float32).astype(ml_dtypes.bfloat16)).reshape(k // 32, 32, n)
    amax = np.abs(w).max(1)
    byte = np.clip(np.where(amax > 0, np.frexp(amax)[1] - 1 + 127 - 7, 1), 1, 254)
    scaled = (w * np.exp2(127.0 - byte)[:, None, :]).reshape(k, n).astype(np.float32)
    words = np.ascontiguousarray(scaled.reshape(k // 512, 128, 4, n).transpose(0, 1, 3, 2)).astype(ml_dtypes.float8_e4m3fn).view(np.uint8)
    return words, np.ascontiguousarray(byte.astype(np.uint8).reshape(k // 512, 16, n))


def unpack_weight(words, scales):
    g, p, n, _ = words.shape
    vals = np.ascontiguousarray(words).view(ml_dtypes.float8_e4m3fn).astype(np.float64) * np.repeat(np.exp2(scales.astype(np.float64) - 127.0), 8, axis=1)[..., None]
    return vals.transpose(0, 1, 3, 2).reshape(g * 512, n)


def relu(v):
    return np.maximum(v, 0.0)

def planes(y):
    n, m = y.shape
    v = y.astype(np.float32).astype(ml_dtypes.bfloat16).astype(np.float64).reshape(n // 32, 32, m)
    top = np.abs(v).max(1)
    byte = np.clip(np.where(top > 0, np.frexp(top)[1] - 1 + 127 - 7, 1), 1, 254)
    codes = (v * np.exp2(127.0 - byte)[:, None, :]).reshape(n, m).astype(np.float32).astype(ml_dtypes.float8_e4m3fn).view(np.uint8)
    words = codes.reshape(n // 512, 128, 4, m).transpose(0, 1, 3, 2)
    return np.ascontiguousarray(words), np.ascontiguousarray(byte.astype(np.uint8).reshape(n // 512, 16, m))


K, T, S, H = 512, 2048, 512, 512


def setup_inputs():
    n = np.random.standard_normal
    s = mx_kscale(K)[:, None]
    u = mx_kscale(H)
    packed_xT = pack_weight(n((K, T)) * s)
    packed_w2 = pack_weight(n((H, H)) / np.sqrt(H) / u[:, None])
    return {
        "x_words": packed_xT[0],
        "x_scales": packed_xT[1],
        "w1": (n((K, H)) / np.sqrt(K) / s * u).astype(np.float32),
        "w2_words": packed_w2[0],
        "w2_scales": packed_w2[1],
        "offs": striped8(np.stack([np.random.permutation(T)[:S] for _ in range(8)])),
    }


def reference(x_words, x_scales, w1, w2_words, w2_scales, offs):
    xq = unpack_weight(x_words, x_scales)[np.arange(K)[:, None], runs(offs, K)]
    h = relu(mxq(f64(w1), 0, "e4m3").T @ xq)
    out_0 = unpack_weight(w2_words, w2_scales).T @ mxq(h, 0, "e4m3")
    return (out_0,) + planes(out_0)

@@ -1,0 +1,182 @@
+from contextlib import ExitStack
+
+import concourse.mybir as mybir
+
+K, T, S, H = 512, 2048, 512, 512
+FLOPS = 2 * K * H * S + 2 * H * H * S
+
+F32 = mybir.dt.float32
+BF16 = mybir.dt.bfloat16
+I32 = mybir.dt.int32
+U32 = mybir.dt.uint32
+U16 = mybir.dt.uint16
+U8 = mybir.dt.uint8
+FP8X4 = mybir.dt.float8_e4m3fn_x4
+RELU = mybir.ActivationFunctionType.Relu
+MAX = mybir.AluOpType.max
+
+P = 128
+PACK = 4
+QUAD = 32
+BLOCK = 128
+BLOCKS = S // BLOCK
+GATHER = 256
+M_SCALAR = 48
+
+
+def tile_picked_phmlp_relu_po_kernel(tc, x_words, x_scales, w1, w2_words, w2_scales, offs, out_0, out_1, out_2):
+    nc = tc.nc
+    with ExitStack() as ctx:
+        keep = ctx.enter_context(tc.tile_pool(name="keep", bufs=1))
+        psum = ctx.enter_context(tc.psum_pool(name="psum", bufs=1))
+
+        offsets = keep.tile([P, S // 16], U16, name="offsets")
+        nc.sync.dma_start(offsets[:], offs)
+
+        w1_raw = keep.tile([P, PACK, H], F32, name="w1_raw")
+        nc.scalar.dma_start(out=w1_raw[:], in_=w1.rearrange("(p j) c -> p j c", j=PACK))
+        xw_table = keep.tile([P, T], U32, name="xw_table")
+        nc.scalar.dma_start(out=xw_table[:].bitcast(I32), in_=x_words[0].rearrange("p n t -> p (n t)").bitcast(I32))
+        w2w_raw = keep.tile([P, H], I32, name="w2w_raw")
+        nc.scalar.dma_start(out=w2w_raw[:], in_=w2_words[0].rearrange("p n t -> p (n t)").bitcast(I32))
+
+        xs_table = keep.tile([P, T], U8, name="xs_table")
+        nc.vector.memset(xs_table[:].bitcast(I32), 0)
+        nc.sync.dma_start(out=xs_table[0:P:8, :].bitcast(I32), in_=x_scales[0].bitcast(I32))
+
+        w2s_raw = keep.tile([P, H], U8, name="w2s_raw")
+        nc.vector.memset(w2s_raw[:].bitcast(I32), 0)
+        x_plane = keep.tile([P, S], U8, name="x_plane", align_bytes=64)
+        nc.vector.memset(x_plane[:].bitcast(I32), 0)
+        for q in range(4):
+            nc.sync.dma_start(
+                out=w2s_raw[QUAD * q : QUAD * q + 4, :].bitcast(I32),
+                in_=w2_scales[0, 4 * q : 4 * q + 4, :].bitcast(I32),
+            )
+
+        xs_picked = keep.tile([P, S], U8, name="xs_picked")
+        nc.vector.tensor_copy(xs_picked[:], xs_table[:].indirect(offsets[:]))
+        for j in range(4):
+            nc.sync.dma_start(
+                out=x_plane[j:P:QUAD, :].bitcast(I32),
+                in_=xs_picked[8 * j : P : QUAD, :].bitcast(I32),
+            )
+
+        w1_bf = keep.tile([P, PACK, P, PACK], BF16, name="w1_bf", align_bytes=64)
+        dst = w1_bf[:].rearrange("p t m j -> p m t j")
+        src = w1_raw[:].rearrange("p j (m t) -> p m t j", t=PACK)
+        nc.scalar.copy(out=dst[:, :M_SCALAR], in_=src[:, :M_SCALAR])
+        nc.vector.tensor_copy(out=dst[:, M_SCALAR:], in_=src[:, M_SCALAR:])
+        w2_plane = keep.tile([P, H], U8, name="w2_plane", align_bytes=64)
+        nc.vector.tensor_copy(
+            out=w2_plane[:].rearrange("p (t m) -> p m t", t=PACK),
+            in_=w2s_raw[:].rearrange("p (m t) -> p m t", t=PACK),
+        )
+        w1_codes = keep.tile([P, H], U32, name="w1_codes", align_bytes=64)
+        w1_plane = keep.tile([P, H], U8, name="w1_plane", align_bytes=64)
+        nc.vector.quantize_mx(
+            out=w1_codes[:].bitcast(FP8X4),
+            scales=w1_plane[:],
+            in_=w1_bf[:].rearrange("p t m j -> p (t m j)"),
+        )
+
+        x_codes = keep.tile([P, S], U32, name="x_codes", align_bytes=64)
+        for g in range(S // GATHER):
+            nc.vector.tensor_copy(
+                x_codes[:, g * GATHER : (g + 1) * GATHER],
+                xw_table[:].indirect(offsets[:, g * GATHER // 16 : (g + 1) * GATHER // 16]),
+            )
+        w2_codes = keep.tile([P, H], I32, name="w2_codes", align_bytes=64)
+        nc.vector.tensor_copy(
+            out=w2_codes[:].rearrange("p (t m) -> p m t", t=PACK),
+            in_=w2w_raw[:].rearrange("p (m t) -> p m t", t=PACK),
+        )
+
+        h_codes = keep.tile([P, S], U32, name="h_codes", align_bytes=64)
+        h_plane = keep.tile([P, S], U8, name="h_plane", align_bytes=64)
+        y_codes = keep.tile([P, S], U32, name="y_codes", align_bytes=64)
+        y_plane = keep.tile([P, S], U8, name="y_plane", align_bytes=64)
+        h_bank = [psum.tile([P, PACK, BLOCK], F32, name="h_bank%d" % b) for b in range(BLOCKS)]
+        y_bank = [psum.tile([P, PACK, BLOCK], F32, name="y_bank%d" % b) for b in range(BLOCKS)]
+        h_bf = [keep.tile([P, BLOCK, PACK], BF16, name="h_bf%d" % b, align_bytes=64) for b in range(BLOCKS)]
+        y_f32 = [keep.tile([P, PACK, BLOCK], F32, name="y_f32%d" % b) for b in range(BLOCKS)]
+        y_bf = [keep.tile([P, BLOCK, PACK], BF16, name="y_bf%d" % b, align_bytes=64) for b in range(BLOCKS)]
+        out_rows = out_0.rearrange("(p t) n -> p t n", t=PACK)
+        out_words = out_1[0].rearrange("p n t -> p (n t)").bitcast(I32)
+
+        def cols(b):
+            return slice(b * BLOCK, (b + 1) * BLOCK)
+
+        def layer(bank, w_codes, w_plane, a_codes, a_plane, b):
+            for t in range(PACK):
+                nc.tensor.matmul_mx(
+                    out=bank[:, t, :],
+                    lhsT=w_codes[:, t * P : (t + 1) * P].bitcast(FP8X4),
+                    lhsT_scale=w_plane[:, t * P : (t + 1) * P],
+                    rhs=a_codes[:, cols(b)].bitcast(FP8X4),
+                    rhs_scale=a_plane[:, cols(b)],
+                    start=True,
+                    stop=True,
+                )
+
+        def first(b):
+            layer(h_bank[b], w1_codes, w1_plane, x_codes, x_plane, b)
+
+        def second(b):
+            layer(y_bank[b], w2_codes, w2_plane, h_codes, h_plane, b)
+
+        def relu(b, on_vector):
+            stepped = h_bank[b][:].rearrange("p t n -> p n t")
+            if on_vector:
+                nc.vector.tensor_scalar(h_bf[b][:], stepped, 0.0, None, MAX)
+            else:
+                nc.scalar.activation(h_bf[b][:], stepped, RELU)
+
+        def quantise(codes, plane, src_bf, b):
+            nc.vector.quantize_mx(
+                out=codes[:, cols(b)].bitcast(FP8X4),
+                scales=plane[:, cols(b)],
+                in_=src_bf[:].rearrange("p n t -> p (n t)"),
+            )
+
+        def result(b):
+            nc.scalar.copy(out=y_f32[b][:], in_=y_bank[b][:])
+            nc.sync.dma_start(out=out_rows[:, :, cols(b)], in_=y_f32[b][:])
+
+        def planes(b):
+            nc.vector.tensor_copy(
+                out=y_bf[b][:].rearrange("p (c i) t -> p c t i", i=4),
+                in_=y_f32[b][:].rearrange("p t (c i) -> p c t i", i=4),
+            )
+            quantise(y_codes, y_plane, y_bf[b], b)
+
+        first(0)
+        relu(0, False)
+        first(1)
+        relu(1, False)
+        quantise(h_codes, h_plane, h_bf[0], 0)
+        first(2)
+        relu(2, False)
+        first(3)
+        second(0)
+        quantise(h_codes, h_plane, h_bf[1], 1)
+        relu(3, True)
+        second(1)
+        result(0)
+        quantise(h_codes, h_plane, h_bf[2], 2)
+        quantise(h_codes, h_plane, h_bf[3], 3)
+        second(2)
+        second(3)
+        for b in range(BLOCKS):
+            if b > 0:
+                result(b)
+            planes(b)
+            if b % 2 == 1:
+                pair = slice((b - 1) * BLOCK, (b + 1) * BLOCK)
+                nc.sync.dma_start(out=out_words[:, pair], in_=y_codes[:, pair].bitcast(I32))
+        for q in range(4):
+            queue = nc.scalar if q % 2 == 0 else nc.sync
+            queue.dma_start(
+                out=out_2[0, 4 * q : 4 * q + 4, :].bitcast(I32),
+                in_=y_plane[QUAD * q : QUAD * q + 4, :].bitcast(I32),
+            )

@@ -21,7 +21,7 @@ QUAD = 32
 BLOCK = 128
 BLOCKS = S // BLOCK
 GATHER = 256
-M_SCALAR = 48
+M_SCALAR = 64
 
 
 def tile_picked_phmlp_relu_po_kernel(tc, x_words, x_scales, w1, w2_words, w2_scales, offs, out_0, out_1, out_2):
@@ -33,8 +33,14 @@ def tile_picked_phmlp_relu_po_kernel(tc, x_words, x_scales, w1, w2_words, w2_sca
         offsets = keep.tile([P, S // 16], U16, name="offsets")
         nc.sync.dma_start(offsets[:], offs)
 
-        w1_raw = keep.tile([P, PACK, H], F32, name="w1_raw")
-        nc.scalar.dma_start(out=w1_raw[:], in_=w1.rearrange("(p j) c -> p j c", j=PACK))
+        w1_rows = w1.rearrange("(p j) c -> p j c", j=PACK)
+        w1_head = keep.tile([P, PACK, PACK * M_SCALAR], F32, name="w1_head")
+        nc.scalar.dma_start(out=w1_head[:], in_=w1_rows[:, :, : PACK * M_SCALAR])
+        w1_rest = keep.tile([P, PACK, H - PACK * M_SCALAR], F32, name="w1_rest")
+        nc.scalar.dma_start(out=w1_rest[:], in_=w1_rows[:, :, PACK * M_SCALAR :])
+        warm = keep.tile([P, 2], F32, name="warm")
+        nc.gpsimd.memset(warm[:, 0:1], 0.0)
+        nc.scalar.activation(warm[:, 1:2], warm[:, 0:1], RELU)
         xw_table = keep.tile([P, T], U32, name="xw_table")
         nc.scalar.dma_start(out=xw_table[:].bitcast(I32), in_=x_words[0].rearrange("p n t -> p (n t)").bitcast(I32))
         w2w_raw = keep.tile([P, H], I32, name="w2w_raw")
@@ -64,14 +70,8 @@ def tile_picked_phmlp_relu_po_kernel(tc, x_words, x_scales, w1, w2_words, w2_sca
 
         w1_bf = keep.tile([P, PACK, P, PACK], BF16, name="w1_bf", align_bytes=64)
         dst = w1_bf[:].rearrange("p t m j -> p m t j")
-        src = w1_raw[:].rearrange("p j (m t) -> p m t j", t=PACK)
-        nc.scalar.copy(out=dst[:, :M_SCALAR], in_=src[:, :M_SCALAR])
-        nc.vector.tensor_copy(out=dst[:, M_SCALAR:], in_=src[:, M_SCALAR:])
-        w2_plane = keep.tile([P, H], U8, name="w2_plane", align_bytes=64)
-        nc.vector.tensor_copy(
-            out=w2_plane[:].rearrange("p (t m) -> p m t", t=PACK),
-            in_=w2s_raw[:].rearrange("p (m t) -> p m t", t=PACK),
-        )
+        nc.scalar.copy(out=dst[:, :M_SCALAR], in_=w1_head[:].rearrange("p j (m t) -> p m t j", t=PACK))
+        nc.vector.tensor_copy(out=dst[:, M_SCALAR:], in_=w1_rest[:].rearrange("p j (m t) -> p m t j", t=PACK))
         w1_codes = keep.tile([P, H], U32, name="w1_codes", align_bytes=64)
         w1_plane = keep.tile([P, H], U8, name="w1_plane", align_bytes=64)
         nc.vector.quantize_mx(
@@ -80,6 +80,11 @@ def tile_picked_phmlp_relu_po_kernel(tc, x_words, x_scales, w1, w2_words, w2_sca
             in_=w1_bf[:].rearrange("p t m j -> p (t m j)"),
         )
 
+        w2_plane = keep.tile([P, H], U8, name="w2_plane", align_bytes=64)
+        nc.vector.tensor_copy(
+            out=w2_plane[:].rearrange("p (t m) -> p m t", t=PACK),
+            in_=w2s_raw[:].rearrange("p (m t) -> p m t", t=PACK),
+        )
         x_codes = keep.tile([P, S], U32, name="x_codes", align_bytes=64)
         for g in range(S // GATHER):
             nc.vector.tensor_copy(
@@ -171,9 +176,9 @@ def tile_picked_phmlp_relu_po_kernel(tc, x_words, x_scales, w1, w2_words, w2_sca
             if b > 0:
                 result(b)
             planes(b)
-            if b % 2 == 1:
-                pair = slice((b - 1) * BLOCK, (b + 1) * BLOCK)
-                nc.sync.dma_start(out=out_words[:, pair], in_=y_codes[:, pair].bitcast(I32))
+            if b >= BLOCKS - 2:
+                done = slice(0, (b + 1) * BLOCK) if b == BLOCKS - 2 else cols(b)
+                nc.sync.dma_start(out=out_words[:, done], in_=y_codes[:, done].bitcast(I32))
         for q in range(4):
             queue = nc.scalar if q % 2 == 0 else nc.sync
             queue.dma_start(

@@ -21,7 +21,7 @@ QUAD = 32
 BLOCK = 128
 BLOCKS = S // BLOCK
 GATHER = 256
-M_SCALAR = 64
+M_SCALAR = 42
 
 
 def tile_picked_phmlp_relu_po_kernel(tc, x_words, x_scales, w1, w2_words, w2_scales, offs, out_0, out_1, out_2):
@@ -33,32 +33,29 @@ def tile_picked_phmlp_relu_po_kernel(tc, x_words, x_scales, w1, w2_words, w2_sca
         offsets = keep.tile([P, S // 16], U16, name="offsets")
         nc.sync.dma_start(offsets[:], offs)
 
-        w1_rows = w1.rearrange("(p j) c -> p j c", j=PACK)
-        w1_head = keep.tile([P, PACK, PACK * M_SCALAR], F32, name="w1_head")
-        nc.scalar.dma_start(out=w1_head[:], in_=w1_rows[:, :, : PACK * M_SCALAR])
-        w1_rest = keep.tile([P, PACK, H - PACK * M_SCALAR], F32, name="w1_rest")
-        nc.scalar.dma_start(out=w1_rest[:], in_=w1_rows[:, :, PACK * M_SCALAR :])
-        warm = keep.tile([P, 2], F32, name="warm")
-        nc.gpsimd.memset(warm[:, 0:1], 0.0)
-        nc.scalar.activation(warm[:, 1:2], warm[:, 0:1], RELU)
-        xw_table = keep.tile([P, T], U32, name="xw_table")
-        nc.scalar.dma_start(out=xw_table[:].bitcast(I32), in_=x_words[0].rearrange("p n t -> p (n t)").bitcast(I32))
-        w2w_raw = keep.tile([P, H], I32, name="w2w_raw")
-        nc.scalar.dma_start(out=w2w_raw[:], in_=w2_words[0].rearrange("p n t -> p (n t)").bitcast(I32))
-
-        xs_table = keep.tile([P, T], U8, name="xs_table")
-        nc.vector.memset(xs_table[:].bitcast(I32), 0)
-        nc.sync.dma_start(out=xs_table[0:P:8, :].bitcast(I32), in_=x_scales[0].bitcast(I32))
-
         w2s_raw = keep.tile([P, H], U8, name="w2s_raw")
         nc.vector.memset(w2s_raw[:].bitcast(I32), 0)
+        xs_table = keep.tile([P, T], U8, name="xs_table", tag="table_then_w2")
+        nc.vector.memset(xs_table[:].bitcast(I32), 0)
         x_plane = keep.tile([P, S], U8, name="x_plane", align_bytes=64)
         nc.vector.memset(x_plane[:].bitcast(I32), 0)
+
+        w1_rows = w1.rearrange("(p j) c -> p j c", j=PACK)
+        w1_raw = keep.tile([P, PACK, H], F32, name="w1_raw")
+        nc.sync.dma_start(out=w1_raw[:, :2], in_=w1_rows[:, :2])
         for q in range(4):
             nc.sync.dma_start(
                 out=w2s_raw[QUAD * q : QUAD * q + 4, :].bitcast(I32),
                 in_=w2_scales[0, 4 * q : 4 * q + 4, :].bitcast(I32),
             )
+        nc.sync.dma_start(out=xs_table[0:P:8, :].bitcast(I32), in_=x_scales[0].bitcast(I32))
+        nc.sync.dma_start(out=w1_raw[:, 2:], in_=w1_rows[:, 2:])
+        xw_table = keep.tile([P, T], U32, name="xw_table", tag="words_then_w2", align_bytes=64)
+        nc.sync.dma_start(out=xw_table[:].bitcast(I32), in_=x_words[0].rearrange("p n t -> p (n t)").bitcast(I32))
+
+        warm = keep.tile([P, 2], F32, name="warm")
+        nc.gpsimd.memset(warm[:, 0:1], 0.0)
+        nc.scalar.activation(warm[:, 1:2], warm[:, 0:1], RELU)
 
         xs_picked = keep.tile([P, S], U8, name="xs_picked")
         nc.vector.tensor_copy(xs_picked[:], xs_table[:].indirect(offsets[:]))
@@ -67,11 +64,14 @@ def tile_picked_phmlp_relu_po_kernel(tc, x_words, x_scales, w1, w2_words, w2_sca
                 out=x_plane[j:P:QUAD, :].bitcast(I32),
                 in_=xs_picked[8 * j : P : QUAD, :].bitcast(I32),
             )
+        w2w_raw = keep.tile([P, 4 * H], U8, name="w2w_raw", tag="table_then_w2")
+        nc.sync.dma_start(out=w2w_raw[:].bitcast(I32), in_=w2_words[0].rearrange("p n t -> p (n t)").bitcast(I32))
 
-        w1_bf = keep.tile([P, PACK, P, PACK], BF16, name="w1_bf", align_bytes=64)
+        w1_bf = keep.tile([P, PACK, P, PACK], BF16, name="w1_bf", tag="w1_then_x", align_bytes=64)
+        src = w1_raw[:].rearrange("p j (m t) -> p m t j", t=PACK)
         dst = w1_bf[:].rearrange("p t m j -> p m t j")
-        nc.scalar.copy(out=dst[:, :M_SCALAR], in_=w1_head[:].rearrange("p j (m t) -> p m t j", t=PACK))
-        nc.vector.tensor_copy(out=dst[:, M_SCALAR:], in_=w1_rest[:].rearrange("p j (m t) -> p m t j", t=PACK))
+        nc.scalar.copy(out=dst[:, :M_SCALAR], in_=src[:, :M_SCALAR])
+        nc.vector.tensor_copy(out=dst[:, M_SCALAR:], in_=src[:, M_SCALAR:])
         w1_codes = keep.tile([P, H], U32, name="w1_codes", align_bytes=64)
         w1_plane = keep.tile([P, H], U8, name="w1_plane", align_bytes=64)
         nc.vector.quantize_mx(
@@ -85,16 +85,16 @@ def tile_picked_phmlp_relu_po_kernel(tc, x_words, x_scales, w1, w2_words, w2_sca
             out=w2_plane[:].rearrange("p (t m) -> p m t", t=PACK),
             in_=w2s_raw[:].rearrange("p (m t) -> p m t", t=PACK),
         )
-        x_codes = keep.tile([P, S], U32, name="x_codes", align_bytes=64)
+        x_codes = keep.tile([P, S], U32, name="x_codes", tag="w1_then_x", align_bytes=64)
         for g in range(S // GATHER):
             nc.vector.tensor_copy(
                 x_codes[:, g * GATHER : (g + 1) * GATHER],
                 xw_table[:].indirect(offsets[:, g * GATHER // 16 : (g + 1) * GATHER // 16]),
             )
-        w2_codes = keep.tile([P, H], I32, name="w2_codes", align_bytes=64)
+        w2_codes = keep.tile([P, H], I32, name="w2_codes", tag="words_then_w2", align_bytes=64)
         nc.vector.tensor_copy(
             out=w2_codes[:].rearrange("p (t m) -> p m t", t=PACK),
-            in_=w2w_raw[:].rearrange("p (m t) -> p m t", t=PACK),
+            in_=w2w_raw[:].bitcast(I32).rearrange("p (m t) -> p m t", t=PACK),
         )
 
         h_codes = keep.tile([P, S], U32, name="h_codes", align_bytes=64)

@@ -21,7 +21,7 @@ QUAD = 32
 BLOCK = 128
 BLOCKS = S // BLOCK
 GATHER = 256
-M_SCALAR = 42
+M_SCALAR = 24
 
 
 def tile_picked_phmlp_relu_po_kernel(tc, x_words, x_scales, w1, w2_words, w2_scales, offs, out_0, out_1, out_2):
@@ -33,23 +33,24 @@ def tile_picked_phmlp_relu_po_kernel(tc, x_words, x_scales, w1, w2_words, w2_sca
         offsets = keep.tile([P, S // 16], U16, name="offsets")
         nc.sync.dma_start(offsets[:], offs)
 
-        w2s_raw = keep.tile([P, H], U8, name="w2s_raw")
-        nc.vector.memset(w2s_raw[:].bitcast(I32), 0)
         xs_table = keep.tile([P, T], U8, name="xs_table", tag="table_then_w2")
         nc.vector.memset(xs_table[:].bitcast(I32), 0)
+        w2s_raw = keep.tile([P, H], U8, name="w2s_raw")
+        nc.vector.memset(w2s_raw[:].bitcast(I32), 0)
         x_plane = keep.tile([P, S], U8, name="x_plane", align_bytes=64)
         nc.vector.memset(x_plane[:].bitcast(I32), 0)
 
         w1_rows = w1.rearrange("(p j) c -> p j c", j=PACK)
-        w1_raw = keep.tile([P, PACK, H], F32, name="w1_raw")
-        nc.sync.dma_start(out=w1_raw[:, :2], in_=w1_rows[:, :2])
+        w1_head = keep.tile([P, PACK, H // 2], F32, name="w1_head")
+        nc.sync.dma_start(out=w1_head[:], in_=w1_rows[:, :, : H // 2])
+        nc.sync.dma_start(out=xs_table[0:P:8, :].bitcast(I32), in_=x_scales[0].bitcast(I32))
+        w1_rest = keep.tile([P, PACK, H // 2], F32, name="w1_rest", tag="rest_then_plane", align_bytes=64)
+        nc.sync.dma_start(out=w1_rest[:], in_=w1_rows[:, :, H // 2 :])
         for q in range(4):
             nc.sync.dma_start(
                 out=w2s_raw[QUAD * q : QUAD * q + 4, :].bitcast(I32),
                 in_=w2_scales[0, 4 * q : 4 * q + 4, :].bitcast(I32),
             )
-        nc.sync.dma_start(out=xs_table[0:P:8, :].bitcast(I32), in_=x_scales[0].bitcast(I32))
-        nc.sync.dma_start(out=w1_raw[:, 2:], in_=w1_rows[:, 2:])
         xw_table = keep.tile([P, T], U32, name="xw_table", tag="words_then_w2", align_bytes=64)
         nc.sync.dma_start(out=xw_table[:].bitcast(I32), in_=x_words[0].rearrange("p n t -> p (n t)").bitcast(I32))
 
@@ -68,10 +69,12 @@ def tile_picked_phmlp_relu_po_kernel(tc, x_words, x_scales, w1, w2_words, w2_sca
         nc.sync.dma_start(out=w2w_raw[:].bitcast(I32), in_=w2_words[0].rearrange("p n t -> p (n t)").bitcast(I32))
 
         w1_bf = keep.tile([P, PACK, P, PACK], BF16, name="w1_bf", tag="w1_then_x", align_bytes=64)
-        src = w1_raw[:].rearrange("p j (m t) -> p m t j", t=PACK)
+        head = w1_head[:].rearrange("p j (m t) -> p m t j", t=PACK)
+        rest = w1_rest[:].rearrange("p j (m t) -> p m t j", t=PACK)
         dst = w1_bf[:].rearrange("p t m j -> p m t j")
-        nc.scalar.copy(out=dst[:, :M_SCALAR], in_=src[:, :M_SCALAR])
-        nc.vector.tensor_copy(out=dst[:, M_SCALAR:], in_=src[:, M_SCALAR:])
+        nc.scalar.copy(out=dst[:, : P // 2], in_=head)
+        nc.scalar.copy(out=dst[:, P // 2 : P // 2 + M_SCALAR], in_=rest[:, :M_SCALAR])
+        nc.vector.tensor_copy(out=dst[:, P // 2 + M_SCALAR :], in_=rest[:, M_SCALAR:])
         w1_codes = keep.tile([P, H], U32, name="w1_codes", align_bytes=64)
         w1_plane = keep.tile([P, H], U8, name="w1_plane", align_bytes=64)
         nc.vector.quantize_mx(
@@ -80,7 +83,7 @@ def tile_picked_phmlp_relu_po_kernel(tc, x_words, x_scales, w1, w2_words, w2_sca
             in_=w1_bf[:].rearrange("p t m j -> p (t m j)"),
         )
 
-        w2_plane = keep.tile([P, H], U8, name="w2_plane", align_bytes=64)
+        w2_plane = keep.tile([P, H], U8, name="w2_plane", tag="rest_then_plane", align_bytes=64)
         nc.vector.tensor_copy(
             out=w2_plane[:].rearrange("p (t m) -> p m t", t=PACK),
             in_=w2s_raw[:].rearrange("p (m t) -> p m t", t=PACK),
@@ -103,7 +106,7 @@ def tile_picked_phmlp_relu_po_kernel(tc, x_words, x_scales, w1, w2_words, w2_sca
         y_plane = keep.tile([P, S], U8, name="y_plane", align_bytes=64)
         h_bank = [psum.tile([P, PACK, BLOCK], F32, name="h_bank%d" % b) for b in range(BLOCKS)]
         y_bank = [psum.tile([P, PACK, BLOCK], F32, name="y_bank%d" % b) for b in range(BLOCKS)]
-        h_bf = [keep.tile([P, BLOCK, PACK], BF16, name="h_bf%d" % b, align_bytes=64) for b in range(BLOCKS)]
+        h_bf = {}
         y_f32 = [keep.tile([P, PACK, BLOCK], F32, name="y_f32%d" % b) for b in range(BLOCKS)]
         y_bf = [keep.tile([P, BLOCK, PACK], BF16, name="y_bf%d" % b, align_bytes=64) for b in range(BLOCKS)]
         out_rows = out_0.rearrange("(p t) n -> p t n", t=PACK)
@@ -131,6 +134,7 @@ def tile_picked_phmlp_relu_po_kernel(tc, x_words, x_scales, w1, w2_words, w2_sca
             layer(y_bank[b], w2_codes, w2_plane, h_codes, h_plane, b)
 
         def relu(b, on_vector):
+            h_bf[b] = keep.tile([P, BLOCK, PACK], BF16, name="h_bf%d" % b, tag="h_bf%d" % (1 if b == 3 else b), align_bytes=64)
             stepped = h_bank[b][:].rearrange("p t n -> p n t")
             if on_vector:
                 nc.vector.tensor_scalar(h_bf[b][:], stepped, 0.0, None, MAX)
@@ -144,41 +148,60 @@ def tile_picked_phmlp_relu_po_kernel(tc, x_words, x_scales, w1, w2_words, w2_sca
                 in_=src_bf[:].rearrange("p n t -> p (n t)"),
             )
 
-        def result(b):
-            nc.scalar.copy(out=y_f32[b][:], in_=y_bank[b][:])
+        def result(b, on_vector):
+            if on_vector:
+                nc.vector.tensor_copy(out=y_f32[b][:], in_=y_bank[b][:])
+            else:
+                nc.scalar.copy(out=y_f32[b][:], in_=y_bank[b][:])
             nc.sync.dma_start(out=out_rows[:, :, cols(b)], in_=y_f32[b][:])
 
-        def planes(b):
+        def rounded(b):
             nc.vector.tensor_copy(
                 out=y_bf[b][:].rearrange("p (c i) t -> p c t i", i=4),
                 in_=y_f32[b][:].rearrange("p t (c i) -> p c t i", i=4),
             )
-            quantise(y_codes, y_plane, y_bf[b], b)
 
+        for bank in y_bank[2:]:
+            nc.tensor.matmul_mx(
+                out=bank[:].rearrange("p t n -> p (t n)"),
+                lhsT=w1_codes[:, :P].bitcast(FP8X4),
+                lhsT_scale=w1_plane[:, :P],
+                rhs=w1_codes[:].bitcast(FP8X4),
+                rhs_scale=w1_plane[:],
+                start=True,
+                stop=True,
+            )
         first(0)
-        relu(0, False)
         first(1)
-        relu(1, False)
-        quantise(h_codes, h_plane, h_bf[0], 0)
+        relu(0, False)
         first(2)
-        relu(2, False)
         first(3)
+        relu(1, True)
+        quantise(h_codes, h_plane, h_bf[0], 0)
+        relu(2, False)
         second(0)
         quantise(h_codes, h_plane, h_bf[1], 1)
-        relu(3, True)
         second(1)
-        result(0)
+        relu(3, True)
         quantise(h_codes, h_plane, h_bf[2], 2)
-        quantise(h_codes, h_plane, h_bf[3], 3)
         second(2)
+        quantise(h_codes, h_plane, h_bf[3], 3)
         second(3)
-        for b in range(BLOCKS):
-            if b > 0:
-                result(b)
-            planes(b)
-            if b >= BLOCKS - 2:
-                done = slice(0, (b + 1) * BLOCK) if b == BLOCKS - 2 else cols(b)
-                nc.sync.dma_start(out=out_words[:, done], in_=y_codes[:, done].bitcast(I32))
+        result(0, False)
+        result(1, False)
+        rounded(0)
+        result(2, False)
+        rounded(1)
+        quantise(y_codes, y_plane, y_bf[0], 0)
+        nc.scalar.copy(out=y_bf[3][:], in_=y_bank[3][:].rearrange("p t n -> p n t"))
+        quantise(y_codes, y_plane, y_bf[1], 1)
+        nc.sync.dma_start(out=out_words[:, : 2 * BLOCK], in_=y_codes[:, : 2 * BLOCK].bitcast(I32))
+        rounded(2)
+        nc.scalar.copy(out=y_f32[3][:], in_=y_bank[3][:])
+        nc.scalar.dma_start(out=out_rows[:, :, cols(3)], in_=y_f32[3][:])
+        quantise(y_codes, y_plane, y_bf[3], 3)
+        quantise(y_codes, y_plane, y_bf[2], 2)
+        nc.sync.dma_start(out=out_words[:, 2 * BLOCK :], in_=y_codes[:, 2 * BLOCK :].bitcast(I32))
         for q in range(4):
             queue = nc.scalar if q % 2 == 0 else nc.sync
             queue.dma_start(

@@ -18,10 +18,12 @@ MAX = mybir.AluOpType.max
 P = 128
 PACK = 4
 QUAD = 32
-BLOCK = 128
-BLOCKS = S // BLOCK
+WIDTHS = (128, 128, 128, 128)
+STARTS = tuple(sum(WIDTHS[:b]) for b in range(len(WIDTHS)))
+BANK = 512
 GATHER = 256
-M_SCALAR = 24
+M_HEAD = 48
+M_SCALAR = 46
 
 
 def tile_picked_phmlp_relu_po_kernel(tc, x_words, x_scales, w1, w2_words, w2_scales, offs, out_0, out_1, out_2):
@@ -30,27 +32,20 @@ def tile_picked_phmlp_relu_po_kernel(tc, x_words, x_scales, w1, w2_words, w2_sca
         keep = ctx.enter_context(tc.tile_pool(name="keep", bufs=1))
         psum = ctx.enter_context(tc.psum_pool(name="psum", bufs=1))
 
-        offsets = keep.tile([P, S // 16], U16, name="offsets")
-        nc.sync.dma_start(offsets[:], offs)
-
-        xs_table = keep.tile([P, T], U8, name="xs_table", tag="table_then_w2")
+        xs_table = keep.tile([P, T], U8, name="xs_table")
         nc.vector.memset(xs_table[:].bitcast(I32), 0)
         w2s_raw = keep.tile([P, H], U8, name="w2s_raw")
         nc.vector.memset(w2s_raw[:].bitcast(I32), 0)
-        x_plane = keep.tile([P, S], U8, name="x_plane", align_bytes=64)
-        nc.vector.memset(x_plane[:].bitcast(I32), 0)
 
         w1_rows = w1.rearrange("(p j) c -> p j c", j=PACK)
-        w1_head = keep.tile([P, PACK, H // 2], F32, name="w1_head")
-        nc.sync.dma_start(out=w1_head[:], in_=w1_rows[:, :, : H // 2])
+        w1_head = keep.tile([P, PACK, PACK * M_HEAD], F32, name="w1_head")
+        nc.sync.dma_start(out=w1_head[:], in_=w1_rows[:, :, : PACK * M_HEAD])
+        offsets = keep.tile([P, S // 16], U16, name="offsets")
+        nc.sync.dma_start(offsets[:], offs)
         nc.sync.dma_start(out=xs_table[0:P:8, :].bitcast(I32), in_=x_scales[0].bitcast(I32))
-        w1_rest = keep.tile([P, PACK, H // 2], F32, name="w1_rest", tag="rest_then_plane", align_bytes=64)
-        nc.sync.dma_start(out=w1_rest[:], in_=w1_rows[:, :, H // 2 :])
-        for q in range(4):
-            nc.sync.dma_start(
-                out=w2s_raw[QUAD * q : QUAD * q + 4, :].bitcast(I32),
-                in_=w2_scales[0, 4 * q : 4 * q + 4, :].bitcast(I32),
-            )
+        nc.sync.dma_start(out=w2s_raw[0:P:8, :].bitcast(I32), in_=w2_scales[0].bitcast(I32))
+        w1_rest = keep.tile([P, PACK, H - PACK * M_HEAD], F32, name="w1_rest")
+        nc.sync.dma_start(out=w1_rest[:], in_=w1_rows[:, :, PACK * M_HEAD :])
         xw_table = keep.tile([P, T], U32, name="xw_table", tag="words_then_w2", align_bytes=64)
         nc.sync.dma_start(out=xw_table[:].bitcast(I32), in_=x_words[0].rearrange("p n t -> p (n t)").bitcast(I32))
 
@@ -58,23 +53,31 @@ def tile_picked_phmlp_relu_po_kernel(tc, x_words, x_scales, w1, w2_words, w2_sca
         nc.gpsimd.memset(warm[:, 0:1], 0.0)
         nc.scalar.activation(warm[:, 1:2], warm[:, 0:1], RELU)
 
-        xs_picked = keep.tile([P, S], U8, name="xs_picked")
+        both_planes = keep.tile([P, S + H], U8, name="both_planes", align_bytes=64)
+        x_plane = both_planes[:, :S]
+        w2_plane = both_planes[:, S:]
+        xs_picked = keep.tile([P, S], U8, name="xs_picked", tag="picked_then_w2")
         nc.vector.tensor_copy(xs_picked[:], xs_table[:].indirect(offsets[:]))
-        for j in range(4):
+        nc.vector.tensor_copy(
+            out=w2_plane.rearrange("p (t m) -> p m t", t=PACK),
+            in_=w2s_raw[:].rearrange("p (m t) -> p m t", t=PACK),
+        )
+        nc.vector.tensor_copy(out=x_plane.bitcast(I32), in_=xs_picked[:].bitcast(I32))
+        for j in range(1, 4):
             nc.sync.dma_start(
-                out=x_plane[j:P:QUAD, :].bitcast(I32),
-                in_=xs_picked[8 * j : P : QUAD, :].bitcast(I32),
+                out=both_planes[j:P:QUAD, :].bitcast(I32),
+                in_=both_planes[8 * j : P : QUAD, :].bitcast(I32),
             )
-        w2w_raw = keep.tile([P, 4 * H], U8, name="w2w_raw", tag="table_then_w2")
+        w2w_raw = keep.tile([P, 4 * H], U8, name="w2w_raw", tag="picked_then_w2")
         nc.sync.dma_start(out=w2w_raw[:].bitcast(I32), in_=w2_words[0].rearrange("p n t -> p (n t)").bitcast(I32))
 
         w1_bf = keep.tile([P, PACK, P, PACK], BF16, name="w1_bf", tag="w1_then_x", align_bytes=64)
         head = w1_head[:].rearrange("p j (m t) -> p m t j", t=PACK)
         rest = w1_rest[:].rearrange("p j (m t) -> p m t j", t=PACK)
         dst = w1_bf[:].rearrange("p t m j -> p m t j")
-        nc.scalar.copy(out=dst[:, : P // 2], in_=head)
-        nc.scalar.copy(out=dst[:, P // 2 : P // 2 + M_SCALAR], in_=rest[:, :M_SCALAR])
-        nc.vector.tensor_copy(out=dst[:, P // 2 + M_SCALAR :], in_=rest[:, M_SCALAR:])
+        nc.scalar.copy(out=dst[:, :M_HEAD], in_=head)
+        nc.scalar.copy(out=dst[:, M_HEAD : M_HEAD + M_SCALAR], in_=rest[:, :M_SCALAR])
+        nc.vector.tensor_copy(out=dst[:, M_HEAD + M_SCALAR :], in_=rest[:, M_SCALAR:])
         w1_codes = keep.tile([P, H], U32, name="w1_codes", align_bytes=64)
         w1_plane = keep.tile([P, H], U8, name="w1_plane", align_bytes=64)
         nc.vector.quantize_mx(
@@ -83,11 +86,6 @@ def tile_picked_phmlp_relu_po_kernel(tc, x_words, x_scales, w1, w2_words, w2_sca
             in_=w1_bf[:].rearrange("p t m j -> p (t m j)"),
         )
 
-        w2_plane = keep.tile([P, H], U8, name="w2_plane", tag="rest_then_plane", align_bytes=64)
-        nc.vector.tensor_copy(
-            out=w2_plane[:].rearrange("p (t m) -> p m t", t=PACK),
-            in_=w2s_raw[:].rearrange("p (m t) -> p m t", t=PACK),
-        )
         x_codes = keep.tile([P, S], U32, name="x_codes", tag="w1_then_x", align_bytes=64)
         for g in range(S // GATHER):
             nc.vector.tensor_copy(
@@ -104,21 +102,24 @@ def tile_picked_phmlp_relu_po_kernel(tc, x_words, x_scales, w1, w2_words, w2_sca
         h_plane = keep.tile([P, S], U8, name="h_plane", align_bytes=64)
         y_codes = keep.tile([P, S], U32, name="y_codes", align_bytes=64)
         y_plane = keep.tile([P, S], U8, name="y_plane", align_bytes=64)
-        h_bank = [psum.tile([P, PACK, BLOCK], F32, name="h_bank%d" % b) for b in range(BLOCKS)]
-        y_bank = [psum.tile([P, PACK, BLOCK], F32, name="y_bank%d" % b) for b in range(BLOCKS)]
+        banks = [psum.tile([P, BANK], F32, name="bank%d" % i) for i in range(8)]
         h_bf = {}
-        y_f32 = [keep.tile([P, PACK, BLOCK], F32, name="y_f32%d" % b) for b in range(BLOCKS)]
-        y_bf = [keep.tile([P, BLOCK, PACK], BF16, name="y_bf%d" % b, align_bytes=64) for b in range(BLOCKS)]
+        y_f32 = [keep.tile([P, PACK, w], F32, name="y_f32%d" % b) for b, w in enumerate(WIDTHS)]
+        y_bf = [keep.tile([P, w, PACK], BF16, name="y_bf%d" % b, align_bytes=64) for b, w in enumerate(WIDTHS)]
         out_rows = out_0.rearrange("(p t) n -> p t n", t=PACK)
         out_words = out_1[0].rearrange("p n t -> p (n t)").bitcast(I32)
 
-        def cols(b):
-            return slice(b * BLOCK, (b + 1) * BLOCK)
+        def cols(b, last=None):
+            last = b if last is None else last
+            return slice(STARTS[b], STARTS[last] + WIDTHS[last])
 
-        def layer(bank, w_codes, w_plane, a_codes, a_plane, b):
+        def view(bank, b):
+            return banks[bank][:, : PACK * WIDTHS[b]].rearrange("p (t n) -> p t n", t=PACK)
+
+        def layer(bank, w_codes, w_plane, a_codes, a_plane, b, upper=None):
             for t in range(PACK):
                 nc.tensor.matmul_mx(
-                    out=bank[:, t, :],
+                    out=view(bank if upper is None or t < 2 else upper, b)[:, t, :],
                     lhsT=w_codes[:, t * P : (t + 1) * P].bitcast(FP8X4),
                     lhsT_scale=w_plane[:, t * P : (t + 1) * P],
                     rhs=a_codes[:, cols(b)].bitcast(FP8X4),
@@ -127,15 +128,23 @@ def tile_picked_phmlp_relu_po_kernel(tc, x_words, x_scales, w1, w2_words, w2_sca
                     stop=True,
                 )
 
-        def first(b):
-            layer(h_bank[b], w1_codes, w1_plane, x_codes, x_plane, b)
+        def first(b, bank):
+            layer(bank, w1_codes, w1_plane, x_codes, x_plane, b)
 
-        def second(b):
-            layer(y_bank[b], w2_codes, w2_plane, h_codes, h_plane, b)
+        def second(b, bank):
+            layer(bank, w2_codes, w2_plane, h_codes, h_plane, b)
 
-        def relu(b, on_vector):
-            h_bf[b] = keep.tile([P, BLOCK, PACK], BF16, name="h_bf%d" % b, tag="h_bf%d" % (1 if b == 3 else b), align_bytes=64)
-            stepped = h_bank[b][:].rearrange("p t n -> p n t")
+        def second_split(b, bank, upper):
+            layer(bank, w2_codes, w2_plane, h_codes, h_plane, b, upper)
+
+        def result_split(b, bank, upper):
+            nc.scalar.copy(out=y_f32[b][:, :2], in_=view(bank, b)[:, :2])
+            nc.vector.tensor_copy(out=y_f32[b][:, 2:], in_=view(upper, b)[:, 2:])
+            nc.sync.dma_start(out=out_rows[:, :, cols(b)], in_=y_f32[b][:])
+
+        def relu(b, bank, on_vector, tag):
+            h_bf[b] = keep.tile([P, WIDTHS[b], PACK], BF16, name="h_bf%d" % b, tag=tag, align_bytes=64)
+            stepped = view(bank, b).rearrange("p t n -> p n t")
             if on_vector:
                 nc.vector.tensor_scalar(h_bf[b][:], stepped, 0.0, None, MAX)
             else:
@@ -145,15 +154,15 @@ def tile_picked_phmlp_relu_po_kernel(tc, x_words, x_scales, w1, w2_words, w2_sca
             nc.vector.quantize_mx(
                 out=codes[:, cols(b)].bitcast(FP8X4),
                 scales=plane[:, cols(b)],
-                in_=src_bf[:].rearrange("p n t -> p (n t)"),
+                in_=src_bf[b][:].rearrange("p n t -> p (n t)"),
             )
 
-        def result(b, on_vector):
+        def result(b, bank, on_vector, queue):
             if on_vector:
-                nc.vector.tensor_copy(out=y_f32[b][:], in_=y_bank[b][:])
+                nc.vector.tensor_copy(out=y_f32[b][:], in_=view(bank, b))
             else:
-                nc.scalar.copy(out=y_f32[b][:], in_=y_bank[b][:])
-            nc.sync.dma_start(out=out_rows[:, :, cols(b)], in_=y_f32[b][:])
+                nc.scalar.copy(out=y_f32[b][:], in_=view(bank, b))
+            queue.dma_start(out=out_rows[:, :, cols(b)], in_=y_f32[b][:])
 
         def rounded(b):
             nc.vector.tensor_copy(
@@ -161,9 +170,15 @@ def tile_picked_phmlp_relu_po_kernel(tc, x_words, x_scales, w1, w2_words, w2_sca
                 in_=y_f32[b][:].rearrange("p t (c i) -> p c t i", i=4),
             )
 
-        for bank in y_bank[2:]:
+        def rounded_from_bank(b, bank):
+            nc.scalar.copy(out=y_bf[b][:], in_=view(bank, b).rearrange("p t n -> p n t"))
+
+        def store_words(b, last):
+            nc.sync.dma_start(out=out_words[:, cols(b, last)], in_=y_codes[:, cols(b, last)].bitcast(I32))
+
+        for bank in banks[6:]:
             nc.tensor.matmul_mx(
-                out=bank[:].rearrange("p t n -> p (t n)"),
+                out=bank[:],
                 lhsT=w1_codes[:, :P].bitcast(FP8X4),
                 lhsT_scale=w1_plane[:, :P],
                 rhs=w1_codes[:].bitcast(FP8X4),
@@ -171,37 +186,36 @@ def tile_picked_phmlp_relu_po_kernel(tc, x_words, x_scales, w1, w2_words, w2_sca
                 start=True,
                 stop=True,
             )
-        first(0)
-        first(1)
-        relu(0, False)
-        first(2)
-        first(3)
-        relu(1, True)
-        quantise(h_codes, h_plane, h_bf[0], 0)
-        relu(2, False)
-        second(0)
-        quantise(h_codes, h_plane, h_bf[1], 1)
-        second(1)
-        relu(3, True)
-        quantise(h_codes, h_plane, h_bf[2], 2)
-        second(2)
-        quantise(h_codes, h_plane, h_bf[3], 3)
-        second(3)
-        result(0, False)
-        result(1, False)
+        first(0, 0)
+        first(1, 1)
+        relu(0, 0, False, "h0")
+        first(2, 2)
+        first(3, 3)
+        relu(1, 1, True, "h1")
+        quantise(h_codes, h_plane, h_bf, 0)
+        relu(2, 2, False, "h2")
+        second_split(0, 4, 0)
+        quantise(h_codes, h_plane, h_bf, 1)
+        second(1, 5)
+        relu(3, 3, False, "h3")
+        quantise(h_codes, h_plane, h_bf, 2)
+        second(2, 6)
+        result_split(0, 4, 0)
+        quantise(h_codes, h_plane, h_bf, 3)
+        second(3, 7)
+        result(1, 5, False, nc.sync)
         rounded(0)
-        result(2, False)
+        result(2, 6, False, nc.sync)
         rounded(1)
-        quantise(y_codes, y_plane, y_bf[0], 0)
-        nc.scalar.copy(out=y_bf[3][:], in_=y_bank[3][:].rearrange("p t n -> p n t"))
-        quantise(y_codes, y_plane, y_bf[1], 1)
-        nc.sync.dma_start(out=out_words[:, : 2 * BLOCK], in_=y_codes[:, : 2 * BLOCK].bitcast(I32))
+        quantise(y_codes, y_plane, y_bf, 0)
+        rounded_from_bank(3, 7)
+        quantise(y_codes, y_plane, y_bf, 1)
+        store_words(0, 1)
         rounded(2)
-        nc.scalar.copy(out=y_f32[3][:], in_=y_bank[3][:])
-        nc.scalar.dma_start(out=out_rows[:, :, cols(3)], in_=y_f32[3][:])
-        quantise(y_codes, y_plane, y_bf[3], 3)
-        quantise(y_codes, y_plane, y_bf[2], 2)
-        nc.sync.dma_start(out=out_words[:, 2 * BLOCK :], in_=y_codes[:, 2 * BLOCK :].bitcast(I32))
+        result(3, 7, False, nc.scalar)
+        quantise(y_codes, y_plane, y_bf, 3)
+        quantise(y_codes, y_plane, y_bf, 2)
+        store_words(2, 3)
         for q in range(4):
             queue = nc.scalar if q % 2 == 0 else nc.sync
             queue.dma_start(

@@ -23,7 +23,7 @@ STARTS = tuple(sum(WIDTHS[:b]) for b in range(len(WIDTHS)))
 BANK = 512
 GATHER = 256
 M_HEAD = 48
-M_SCALAR = 46
+M_SCALAR = 38
 
 
 def tile_picked_phmlp_relu_po_kernel(tc, x_words, x_scales, w1, w2_words, w2_scales, offs, out_0, out_1, out_2):
@@ -80,11 +80,12 @@ def tile_picked_phmlp_relu_po_kernel(tc, x_words, x_scales, w1, w2_words, w2_sca
         nc.vector.tensor_copy(out=dst[:, M_HEAD + M_SCALAR :], in_=rest[:, M_SCALAR:])
         w1_codes = keep.tile([P, H], U32, name="w1_codes", align_bytes=64)
         w1_plane = keep.tile([P, H], U8, name="w1_plane", align_bytes=64)
-        nc.vector.quantize_mx(
-            out=w1_codes[:].bitcast(FP8X4),
-            scales=w1_plane[:],
-            in_=w1_bf[:].rearrange("p t m j -> p (t m j)"),
-        )
+        for half in range(2):
+            nc.vector.quantize_mx(
+                out=w1_codes[:, half * 2 * P : (half + 1) * 2 * P].bitcast(FP8X4),
+                scales=w1_plane[:, half * 2 * P : (half + 1) * 2 * P],
+                in_=w1_bf[:, half * 2 : (half + 1) * 2].rearrange("p t m j -> p (t m j)"),
+            )
 
         x_codes = keep.tile([P, S], U32, name="x_codes", tag="w1_then_x", align_bytes=64)
         for g in range(S // GATHER):
@@ -176,13 +177,13 @@ def tile_picked_phmlp_relu_po_kernel(tc, x_words, x_scales, w1, w2_words, w2_sca
         def store_words(b, last):
             nc.sync.dma_start(out=out_words[:, cols(b, last)], in_=y_codes[:, cols(b, last)].bitcast(I32))
 
-        for bank in banks[6:]:
+        for bank, width in ((5, 2 * P), (6, 2 * P), (7, H)):
             nc.tensor.matmul_mx(
-                out=bank[:],
+                out=banks[bank][:, :width],
                 lhsT=w1_codes[:, :P].bitcast(FP8X4),
                 lhsT_scale=w1_plane[:, :P],
-                rhs=w1_codes[:].bitcast(FP8X4),
-                rhs_scale=w1_plane[:],
+                rhs=w1_codes[:, :width].bitcast(FP8X4),
+                rhs_scale=w1_plane[:, :width],
                 start=True,
                 stop=True,
             )

@@ -200,13 +200,13 @@ def tile_picked_phmlp_relu_po_kernel(tc, x_words, x_scales, w1, w2_words, w2_sca
         second(1, 5)
         relu(3, 3, False, "h3")
         quantise(h_codes, h_plane, h_bf, 2)
-        second(2, 6)
+        second_split(2, 6, 1)
         result_split(0, 4, 0)
         quantise(h_codes, h_plane, h_bf, 3)
         second(3, 7)
         result(1, 5, False, nc.sync)
         rounded(0)
-        result(2, 6, False, nc.sync)
+        result_split(2, 6, 1)
         rounded(1)
         quantise(y_codes, y_plane, y_bf, 0)
         rounded_from_bank(3, 7)

@@ -32,10 +32,11 @@ def tile_picked_phmlp_relu_po_kernel(tc, x_words, x_scales, w1, w2_words, w2_sca
         keep = ctx.enter_context(tc.tile_pool(name="keep", bufs=1))
         psum = ctx.enter_context(tc.psum_pool(name="psum", bufs=1))
 
-        xs_table = keep.tile([P, T], U8, name="xs_table")
-        nc.vector.memset(xs_table[:].bitcast(I32), 0)
         w2s_raw = keep.tile([P, H], U8, name="w2s_raw")
         nc.vector.memset(w2s_raw[:].bitcast(I32), 0)
+        nc.scalar.dma_start(out=w2s_raw[0:P:8, :].bitcast(I32), in_=w2_scales[0].bitcast(I32))
+        xs_table = keep.tile([P, T], U8, name="xs_table")
+        nc.vector.memset(xs_table[:].bitcast(I32), 0)
 
         w1_rows = w1.rearrange("(p j) c -> p j c", j=PACK)
         w1_head = keep.tile([P, PACK, PACK * M_HEAD], F32, name="w1_head")
@@ -43,7 +44,6 @@ def tile_picked_phmlp_relu_po_kernel(tc, x_words, x_scales, w1, w2_words, w2_sca
         offsets = keep.tile([P, S // 16], U16, name="offsets")
         nc.sync.dma_start(offsets[:], offs)
         nc.sync.dma_start(out=xs_table[0:P:8, :].bitcast(I32), in_=x_scales[0].bitcast(I32))
-        nc.sync.dma_start(out=w2s_raw[0:P:8, :].bitcast(I32), in_=w2_scales[0].bitcast(I32))
         w1_rest = keep.tile([P, PACK, H - PACK * M_HEAD], F32, name="w1_rest")
         nc.sync.dma_start(out=w1_rest[:], in_=w1_rows[:, :, PACK * M_HEAD :])
         xw_table = keep.tile([P, T], U32, name="xw_table", tag="words_then_w2", align_bytes=64)
@@ -56,12 +56,12 @@ def tile_picked_phmlp_relu_po_kernel(tc, x_words, x_scales, w1, w2_words, w2_sca
         both_planes = keep.tile([P, S + H], U8, name="both_planes", align_bytes=64)
         x_plane = both_planes[:, :S]
         w2_plane = both_planes[:, S:]
-        xs_picked = keep.tile([P, S], U8, name="xs_picked", tag="picked_then_w2")
-        nc.vector.tensor_copy(xs_picked[:], xs_table[:].indirect(offsets[:]))
         nc.vector.tensor_copy(
             out=w2_plane.rearrange("p (t m) -> p m t", t=PACK),
             in_=w2s_raw[:].rearrange("p (m t) -> p m t", t=PACK),
         )
+        xs_picked = keep.tile([P, S], U8, name="xs_picked", tag="picked_then_w2")
+        nc.vector.tensor_copy(xs_picked[:], xs_table[:].indirect(offsets[:]))
         nc.vector.tensor_copy(out=x_plane.bitcast(I32), in_=xs_picked[:].bitcast(I32))
         for j in range(1, 4):
             nc.sync.dma_start(
@@ -208,18 +208,16 @@ def tile_picked_phmlp_relu_po_kernel(tc, x_words, x_scales, w1, w2_words, w2_sca
         rounded(0)
         result_split(2, 6, 1)
         rounded(1)
+        result(3, 7, False, nc.sync)
+        rounded(2)
         quantise(y_codes, y_plane, y_bf, 0)
         rounded_from_bank(3, 7)
         quantise(y_codes, y_plane, y_bf, 1)
-        store_words(0, 1)
-        rounded(2)
-        result(3, 7, False, nc.scalar)
-        quantise(y_codes, y_plane, y_bf, 3)
         quantise(y_codes, y_plane, y_bf, 2)
-        store_words(2, 3)
+        quantise(y_codes, y_plane, y_bf, 3)
+        store_words(0, 3)
         for q in range(4):
-            queue = nc.scalar if q % 2 == 0 else nc.sync
-            queue.dma_start(
+            nc.scalar.dma_start(
                 out=out_2[0, 4 * q : 4 * q + 4, :].bitcast(I32),
                 in_=y_plane[QUAD * q : QUAD * q + 4, :].bitcast(I32),
             )

@@ -23,7 +23,6 @@ STARTS = tuple(sum(WIDTHS[:b]) for b in range(len(WIDTHS)))
 BANK = 512
 GATHER = 256
 M_HEAD = 48
-M_SCALAR = 38
 
 
 def tile_picked_phmlp_relu_po_kernel(tc, x_words, x_scales, w1, w2_words, w2_scales, offs, out_0, out_1, out_2):
@@ -53,6 +52,11 @@ def tile_picked_phmlp_relu_po_kernel(tc, x_words, x_scales, w1, w2_words, w2_sca
         nc.gpsimd.memset(warm[:, 0:1], 0.0)
         nc.scalar.activation(warm[:, 1:2], warm[:, 0:1], RELU)
 
+        w1_bf = keep.tile([P, PACK, P, PACK], BF16, name="w1_bf", tag="w1_then_x", align_bytes=64)
+        head = w1_head[:].rearrange("p j (m t) -> p m t j", t=PACK)
+        rest = w1_rest[:].rearrange("p j (m t) -> p m t j", t=PACK)
+        dst = w1_bf[:].rearrange("p t m j -> p m t j")
+        nc.scalar.copy(out=dst[:, :M_HEAD], in_=head)
         both_planes = keep.tile([P, S + H], U8, name="both_planes", align_bytes=64)
         x_plane = both_planes[:, :S]
         w2_plane = both_planes[:, S:]
@@ -64,20 +68,14 @@ def tile_picked_phmlp_relu_po_kernel(tc, x_words, x_scales, w1, w2_words, w2_sca
         nc.vector.tensor_copy(xs_picked[:], xs_table[:].indirect(offsets[:]))
         nc.vector.tensor_copy(out=x_plane.bitcast(I32), in_=xs_picked[:].bitcast(I32))
         for j in range(1, 4):
-            nc.sync.dma_start(
+            nc.scalar.dma_start(
                 out=both_planes[j:P:QUAD, :].bitcast(I32),
                 in_=both_planes[8 * j : P : QUAD, :].bitcast(I32),
             )
         w2w_raw = keep.tile([P, 4 * H], U8, name="w2w_raw", tag="picked_then_w2")
         nc.sync.dma_start(out=w2w_raw[:].bitcast(I32), in_=w2_words[0].rearrange("p n t -> p (n t)").bitcast(I32))
 
-        w1_bf = keep.tile([P, PACK, P, PACK], BF16, name="w1_bf", tag="w1_then_x", align_bytes=64)
-        head = w1_head[:].rearrange("p j (m t) -> p m t j", t=PACK)
-        rest = w1_rest[:].rearrange("p j (m t) -> p m t j", t=PACK)
-        dst = w1_bf[:].rearrange("p t m j -> p m t j")
-        nc.scalar.copy(out=dst[:, :M_HEAD], in_=head)
-        nc.scalar.copy(out=dst[:, M_HEAD : M_HEAD + M_SCALAR], in_=rest[:, :M_SCALAR])
-        nc.vector.tensor_copy(out=dst[:, M_HEAD + M_SCALAR :], in_=rest[:, M_SCALAR:])
+        nc.vector.tensor_copy(out=dst[:, M_HEAD:], in_=rest)
         w1_codes = keep.tile([P, H], U32, name="w1_codes", align_bytes=64)
         w1_plane = keep.tile([P, H], U8, name="w1_plane", align_bytes=64)
         for half in range(2):

@@ -175,16 +175,6 @@ def tile_picked_phmlp_relu_po_kernel(tc, x_words, x_scales, w1, w2_words, w2_sca
         def store_words(b, last):
             nc.sync.dma_start(out=out_words[:, cols(b, last)], in_=y_codes[:, cols(b, last)].bitcast(I32))
 
-        for bank, width in ((5, 2 * P), (6, 2 * P), (7, H)):
-            nc.tensor.matmul_mx(
-                out=banks[bank][:, :width],
-                lhsT=w1_codes[:, :P].bitcast(FP8X4),
-                lhsT_scale=w1_plane[:, :P],
-                rhs=w1_codes[:, :width].bitcast(FP8X4),
-                rhs_scale=w1_plane[:, :width],
-                start=True,
-                stop=True,
-            )
         first(0, 0)
         first(1, 1)
         relu(0, 0, False, "h0")

@@ -22,49 +22,45 @@ WIDTHS = (128, 128, 128, 128)
 STARTS = tuple(sum(WIDTHS[:b]) for b in range(len(WIDTHS)))
 BANK = 512
 GATHER = 256
-M_HEAD = 48
+X_HEAD = 640
+HALF = 64
+PIECES = ((0, 64), (64, 96), (96, 128))
 
 
 def tile_picked_phmlp_relu_po_kernel(tc, x_words, x_scales, w1, w2_words, w2_scales, offs, out_0, out_1, out_2):
     nc = tc.nc
     with ExitStack() as ctx:
         keep = ctx.enter_context(tc.tile_pool(name="keep", bufs=1))
+        shared = ctx.enter_context(tc.tile_pool(name="shared", bufs=1))
         psum = ctx.enter_context(tc.psum_pool(name="psum", bufs=1))
-
-        w2s_raw = keep.tile([P, H], U8, name="w2s_raw")
-        nc.vector.memset(w2s_raw[:].bitcast(I32), 0)
-        nc.scalar.dma_start(out=w2s_raw[0:P:8, :].bitcast(I32), in_=w2_scales[0].bitcast(I32))
-        xs_table = keep.tile([P, T], U8, name="xs_table")
-        nc.vector.memset(xs_table[:].bitcast(I32), 0)
-
-        w1_rows = w1.rearrange("(p j) c -> p j c", j=PACK)
-        w1_head = keep.tile([P, PACK, PACK * M_HEAD], F32, name="w1_head")
-        nc.sync.dma_start(out=w1_head[:], in_=w1_rows[:, :, : PACK * M_HEAD])
-        offsets = keep.tile([P, S // 16], U16, name="offsets")
-        nc.sync.dma_start(offsets[:], offs)
-        nc.sync.dma_start(out=xs_table[0:P:8, :].bitcast(I32), in_=x_scales[0].bitcast(I32))
-        w1_rest = keep.tile([P, PACK, H - PACK * M_HEAD], F32, name="w1_rest")
-        nc.sync.dma_start(out=w1_rest[:], in_=w1_rows[:, :, PACK * M_HEAD :])
-        xw_table = keep.tile([P, T], U32, name="xw_table", tag="words_then_w2", align_bytes=64)
-        nc.sync.dma_start(out=xw_table[:].bitcast(I32), in_=x_words[0].rearrange("p n t -> p (n t)").bitcast(I32))
 
         warm = keep.tile([P, 2], F32, name="warm")
         nc.gpsimd.memset(warm[:, 0:1], 0.0)
         nc.scalar.activation(warm[:, 1:2], warm[:, 0:1], RELU)
 
-        w1_bf = keep.tile([P, PACK, P, PACK], BF16, name="w1_bf", tag="w1_then_x", align_bytes=64)
-        head = w1_head[:].rearrange("p j (m t) -> p m t j", t=PACK)
-        rest = w1_rest[:].rearrange("p j (m t) -> p m t j", t=PACK)
-        dst = w1_bf[:].rearrange("p t m j -> p m t j")
-        nc.scalar.copy(out=dst[:, :M_HEAD], in_=head)
         both_planes = keep.tile([P, S + H], U8, name="both_planes", align_bytes=64)
         x_plane = both_planes[:, :S]
-        w2_plane = both_planes[:, S:]
-        nc.vector.tensor_copy(
-            out=w2_plane.rearrange("p (t m) -> p m t", t=PACK),
-            in_=w2s_raw[:].rearrange("p (m t) -> p m t", t=PACK),
-        )
-        xs_picked = keep.tile([P, S], U8, name="xs_picked", tag="picked_then_w2")
+        w2s_raw = both_planes[:, S:]
+        nc.gpsimd.memset(w2s_raw.bitcast(I32), 0)
+        nc.scalar.dma_start(out=both_planes[0:P:8, S:].bitcast(I32), in_=w2_scales[0].bitcast(I32))
+        xs_table = keep.tile([P, T], U8, name="xs_table")
+        nc.vector.memset(xs_table[:].bitcast(I32), 0)
+
+        x_rows = x_words[0].rearrange("p n t -> p (n t)").bitcast(I32)
+        xw_table = keep.tile([P, T], U32, name="xw_table")
+        nc.sync.dma_start(out=xw_table[:, :X_HEAD].bitcast(I32), in_=x_rows[:, :X_HEAD])
+        offsets = keep.tile([P, S // 16], U16, name="offsets")
+        nc.sync.dma_start(offsets[:], offs)
+        nc.sync.dma_start(out=xs_table[0:P:8, :].bitcast(I32), in_=x_scales[0].bitcast(I32))
+        nc.sync.dma_start(out=xw_table[:, X_HEAD:].bitcast(I32), in_=x_rows[:, X_HEAD:])
+        w1_rows = w1.rearrange("(p j) c -> p j c", j=PACK)
+        w1_raw = []
+        for i, (m0, m1) in enumerate(PIECES):
+            piece = keep.tile([P, PACK, PACK * (m1 - m0)], F32, name="w1_raw%d" % i)
+            nc.sync.dma_start(out=piece[:], in_=w1_rows[:, :, PACK * m0 : PACK * m1])
+            w1_raw.append(piece)
+
+        xs_picked = keep.tile([P, S], U8, name="xs_picked", align_bytes=64)
         nc.vector.tensor_copy(xs_picked[:], xs_table[:].indirect(offsets[:]))
         nc.vector.tensor_copy(out=x_plane.bitcast(I32), in_=xs_picked[:].bitcast(I32))
         for j in range(1, 4):
@@ -72,26 +68,49 @@ def tile_picked_phmlp_relu_po_kernel(tc, x_words, x_scales, w1, w2_words, w2_sca
                 out=both_planes[j:P:QUAD, :].bitcast(I32),
                 in_=both_planes[8 * j : P : QUAD, :].bitcast(I32),
             )
-        w2w_raw = keep.tile([P, 4 * H], U8, name="w2w_raw", tag="picked_then_w2")
-        nc.sync.dma_start(out=w2w_raw[:].bitcast(I32), in_=w2_words[0].rearrange("p n t -> p (n t)").bitcast(I32))
 
-        nc.vector.tensor_copy(out=dst[:, M_HEAD:], in_=rest)
-        w1_codes = keep.tile([P, H], U32, name="w1_codes", align_bytes=64)
-        w1_plane = keep.tile([P, H], U8, name="w1_plane", align_bytes=64)
-        for half in range(2):
-            nc.vector.quantize_mx(
-                out=w1_codes[:, half * 2 * P : (half + 1) * 2 * P].bitcast(FP8X4),
-                scales=w1_plane[:, half * 2 * P : (half + 1) * 2 * P],
-                in_=w1_bf[:, half * 2 : (half + 1) * 2].rearrange("p t m j -> p (t m j)"),
-            )
-
-        x_codes = keep.tile([P, S], U32, name="x_codes", tag="w1_then_x", align_bytes=64)
+        x_codes = keep.tile([P, S], U32, name="x_codes", align_bytes=64)
         for g in range(S // GATHER):
             nc.vector.tensor_copy(
                 x_codes[:, g * GATHER : (g + 1) * GATHER],
                 xw_table[:].indirect(offsets[:, g * GATHER // 16 : (g + 1) * GATHER // 16]),
             )
-        w2_codes = keep.tile([P, H], I32, name="w2_codes", tag="words_then_w2", align_bytes=64)
+
+        w2w_raw = keep.tile([P, 4 * H], U8, name="w2w_raw")
+        nc.sync.dma_start(out=w2w_raw[:].bitcast(I32), in_=w2_words[0].rearrange("p n t -> p (n t)").bitcast(I32))
+
+        w1_codes = keep.tile([P, H], U32, name="w1_codes", align_bytes=64)
+        w1_plane = keep.tile([P, H], U8, name="w1_plane", align_bytes=64)
+        w1_bf = [shared.tile([P, PACK, HALF, PACK], BF16, name="w1_bf%d" % half, align_bytes=64, offset=4096 * half) for half in range(2)]
+
+        def round_w1(i, on_scalar):
+            m0, m1 = PIECES[i]
+            src = w1_raw[i][:].rearrange("p j (m t) -> p m t j", t=PACK)
+            dst = w1_bf[m0 // HALF][:].rearrange("p t m j -> p m t j")[:, m0 % HALF : m0 % HALF + m1 - m0]
+            nc.scalar.copy(out=dst[:, :on_scalar], in_=src[:, :on_scalar])
+            if on_scalar < m1 - m0:
+                nc.vector.tensor_copy(out=dst[:, on_scalar:], in_=src[:, on_scalar:])
+
+        def quantise_w1(half):
+            for t in range(PACK):
+                c0 = t * P + half * HALF
+                nc.vector.quantize_mx(
+                    out=w1_codes[:, c0 : c0 + HALF].bitcast(FP8X4),
+                    scales=w1_plane[:, c0 : c0 + HALF],
+                    in_=w1_bf[half][:, t].rearrange("p m j -> p (m j)"),
+                )
+
+        round_w1(0, 24)
+        quantise_w1(0)
+        round_w1(1, 24)
+        round_w1(2, 8)
+        quantise_w1(1)
+        w2_plane = shared.tile([P, H], U8, name="w2_plane", align_bytes=64, offset=4096)
+        nc.vector.tensor_copy(
+            out=w2_plane[:].rearrange("p (t m) -> p t m", t=PACK),
+            in_=w2s_raw.rearrange("p (m t) -> p t m", t=PACK),
+        )
+        w2_codes = shared.tile([P, H], I32, name="w2_codes", align_bytes=64, offset=4096 + H)
         nc.vector.tensor_copy(
             out=w2_codes[:].rearrange("p (t m) -> p m t", t=PACK),
             in_=w2w_raw[:].bitcast(I32).rearrange("p (m t) -> p m t", t=PACK),
@@ -175,6 +194,16 @@ def tile_picked_phmlp_relu_po_kernel(tc, x_words, x_scales, w1, w2_words, w2_sca
         def store_words(b, last):
             nc.sync.dma_start(out=out_words[:, cols(b, last)], in_=y_codes[:, cols(b, last)].bitcast(I32))
 
+        for bank, c0, c1 in ((5, 0, GATHER), (6, GATHER, S), (7, 0, S)):
+            nc.tensor.matmul_mx(
+                out=banks[bank][:, : c1 - c0],
+                lhsT=x_codes[:, :P].bitcast(FP8X4),
+                lhsT_scale=xs_picked[:, :P],
+                rhs=x_codes[:, c0:c1].bitcast(FP8X4),
+                rhs_scale=xs_picked[:, c0:c1],
+                start=True,
+                stop=True,
+            )
         first(0, 0)
         first(1, 1)
         relu(0, 0, False, "h0")

@@ -194,13 +194,13 @@ def tile_picked_phmlp_relu_po_kernel(tc, x_words, x_scales, w1, w2_words, w2_sca
         def store_words(b, last):
             nc.sync.dma_start(out=out_words[:, cols(b, last)], in_=y_codes[:, cols(b, last)].bitcast(I32))
 
-        for bank, c0, c1 in ((5, 0, GATHER), (6, GATHER, S), (7, 0, S)):
+        for bank, rows, width in ((5, P, GATHER), (6, HALF, S), (7, HALF, S)):
             nc.tensor.matmul_mx(
-                out=banks[bank][:, : c1 - c0],
-                lhsT=x_codes[:, :P].bitcast(FP8X4),
-                lhsT_scale=xs_picked[:, :P],
-                rhs=x_codes[:, c0:c1].bitcast(FP8X4),
-                rhs_scale=xs_picked[:, c0:c1],
+                out=banks[bank][:rows, :width],
+                lhsT=x_codes[:, :rows].bitcast(FP8X4),
+                lhsT_scale=xs_picked[:, :rows],
+                rhs=x_codes[:, :width].bitcast(FP8X4),
+                rhs_scale=xs_picked[:, :width],
                 start=True,
                 stop=True,
             )

@@ -83,13 +83,13 @@ def tile_picked_phmlp_relu_po_kernel(tc, x_words, x_scales, w1, w2_words, w2_sca
         w1_plane = keep.tile([P, H], U8, name="w1_plane", align_bytes=64)
         w1_bf = [shared.tile([P, PACK, HALF, PACK], BF16, name="w1_bf%d" % half, align_bytes=64, offset=4096 * half) for half in range(2)]
 
-        def round_w1(i, on_scalar):
+        def round_w1(i, on_scalar, tiles_a_copy):
             m0, m1 = PIECES[i]
             src = w1_raw[i][:].rearrange("p j (m t) -> p m t j", t=PACK)
             dst = w1_bf[m0 // HALF][:].rearrange("p t m j -> p m t j")[:, m0 % HALF : m0 % HALF + m1 - m0]
             nc.scalar.copy(out=dst[:, :on_scalar], in_=src[:, :on_scalar])
-            if on_scalar < m1 - m0:
-                nc.vector.tensor_copy(out=dst[:, on_scalar:], in_=src[:, on_scalar:])
+            for t0 in range(0, PACK, tiles_a_copy):
+                nc.vector.tensor_copy(out=dst[:, on_scalar:, t0 : t0 + tiles_a_copy], in_=src[:, on_scalar:, t0 : t0 + tiles_a_copy])
 
         def quantise_w1(half):
             for t in range(PACK):
@@ -100,10 +100,10 @@ def tile_picked_phmlp_relu_po_kernel(tc, x_words, x_scales, w1, w2_words, w2_sca
                     in_=w1_bf[half][:, t].rearrange("p m j -> p (m j)"),
                 )
 
-        round_w1(0, 24)
+        round_w1(0, 24, 4)
         quantise_w1(0)
-        round_w1(1, 24)
-        round_w1(2, 8)
+        round_w1(1, 24, 4)
+        round_w1(2, 8, 2)
         quantise_w1(1)
         w2_plane = shared.tile([P, H], U8, name="w2_plane", align_bytes=64, offset=4096)
         nc.vector.tensor_copy(
@@ -155,9 +155,10 @@ def tile_picked_phmlp_relu_po_kernel(tc, x_words, x_scales, w1, w2_words, w2_sca
         def second_split(b, bank, upper):
             layer(bank, w2_codes, w2_plane, h_codes, h_plane, b, upper)
 
-        def result_split(b, bank, upper):
-            nc.scalar.copy(out=y_f32[b][:, :2], in_=view(bank, b)[:, :2])
-            nc.vector.tensor_copy(out=y_f32[b][:, 2:], in_=view(upper, b)[:, 2:])
+        def result_split(b, bank, upper, vector_first):
+            early, late = (nc.vector.tensor_copy, nc.scalar.copy) if vector_first else (nc.scalar.copy, nc.vector.tensor_copy)
+            early(out=y_f32[b][:, :2], in_=view(bank, b)[:, :2])
+            late(out=y_f32[b][:, 2:], in_=view(upper, b)[:, 2:])
             nc.sync.dma_start(out=out_rows[:, :, cols(b)], in_=y_f32[b][:])
 
         def relu(b, bank, on_vector, tag):
@@ -218,12 +219,12 @@ def tile_picked_phmlp_relu_po_kernel(tc, x_words, x_scales, w1, w2_words, w2_sca
         relu(3, 3, False, "h3")
         quantise(h_codes, h_plane, h_bf, 2)
         second_split(2, 6, 1)
-        result_split(0, 4, 0)
+        result_split(0, 4, 0, True)
         quantise(h_codes, h_plane, h_bf, 3)
         second(3, 7)
         result(1, 5, False, nc.sync)
         rounded(0)
-        result_split(2, 6, 1)
+        result_split(2, 6, 1, False)
         rounded(1)
         result(3, 7, False, nc.sync)
         rounded(2)

@@ -18,13 +18,13 @@ MAX = mybir.AluOpType.max
 P = 128
 PACK = 4
 QUAD = 32
-WIDTHS = (128, 128, 128, 128)
-STARTS = tuple(sum(WIDTHS[:b]) for b in range(len(WIDTHS)))
+GROUP = 128
+GROUPS = S // GROUP
 BANK = 512
 GATHER = 256
-X_HEAD = 640
-HALF = 64
-PIECES = ((0, 64), (64, 96), (96, 128))
+PIECES = ((0, 32), (32, 64), (64, 96), (96, 128))
+SCALAR_SHARES = (0, 32, 32, 10)
+WARM_COLUMNS = 32
 
 
 def tile_picked_phmlp_relu_po_kernel(tc, x_words, x_scales, w1, w2_words, w2_scales, offs, out_0, out_1, out_2):
@@ -38,36 +38,76 @@ def tile_picked_phmlp_relu_po_kernel(tc, x_words, x_scales, w1, w2_words, w2_sca
         nc.gpsimd.memset(warm[:, 0:1], 0.0)
         nc.scalar.activation(warm[:, 1:2], warm[:, 0:1], RELU)
 
-        both_planes = keep.tile([P, S + H], U8, name="both_planes", align_bytes=64)
-        x_plane = both_planes[:, :S]
-        w2s_raw = both_planes[:, S:]
-        nc.gpsimd.memset(w2s_raw.bitcast(I32), 0)
-        nc.scalar.dma_start(out=both_planes[0:P:8, S:].bitcast(I32), in_=w2_scales[0].bitcast(I32))
+        x_plane = shared.tile([P, S], U8, name="x_plane", align_bytes=64, offset=12288)
+        w2s_raw = keep.tile([P, H], U8, name="w2s_raw")
         xs_table = keep.tile([P, T], U8, name="xs_table")
         nc.vector.memset(xs_table[:].bitcast(I32), 0)
+        nc.vector.memset(w2s_raw[:].bitcast(I32), 0)
+        nc.scalar.dma_start(out=w2s_raw[0:P:8, :].bitcast(I32), in_=w2_scales[0].bitcast(I32))
 
-        x_rows = x_words[0].rearrange("p n t -> p (n t)").bitcast(I32)
-        xw_table = keep.tile([P, T], U32, name="xw_table")
-        nc.sync.dma_start(out=xw_table[:, :X_HEAD].bitcast(I32), in_=x_rows[:, :X_HEAD])
+        w1_rows = w1.rearrange("(p j) c -> p j c", j=PACK)
+        w1_raw = [
+            shared.tile([P, PACK, PACK * (m1 - m0)], F32, name="w1_raw%d" % i, align_bytes=64, offset=12288 + 16 * PACK * (P - m1))
+            for i, (m0, m1) in enumerate(PIECES)
+        ]
+
+        def load_w1(i):
+            m0, m1 = PIECES[i]
+            nc.sync.dma_start(out=w1_raw[i][:], in_=w1_rows[:, :, PACK * m0 : PACK * m1])
+
+        load_w1(0)
+        load_w1(1)
         offsets = keep.tile([P, S // 16], U16, name="offsets")
         nc.sync.dma_start(offsets[:], offs)
         nc.sync.dma_start(out=xs_table[0:P:8, :].bitcast(I32), in_=x_scales[0].bitcast(I32))
-        nc.sync.dma_start(out=xw_table[:, X_HEAD:].bitcast(I32), in_=x_rows[:, X_HEAD:])
-        w1_rows = w1.rearrange("(p j) c -> p j c", j=PACK)
-        w1_raw = []
-        for i, (m0, m1) in enumerate(PIECES):
-            piece = keep.tile([P, PACK, PACK * (m1 - m0)], F32, name="w1_raw%d" % i)
-            nc.sync.dma_start(out=piece[:], in_=w1_rows[:, :, PACK * m0 : PACK * m1])
-            w1_raw.append(piece)
+        load_w1(2)
+        load_w1(3)
+        xw_table = keep.tile([P, T], U32, name="xw_table")
+        nc.sync.dma_start(out=xw_table[:].bitcast(I32), in_=x_words[0].rearrange("p n t -> p (n t)").bitcast(I32))
 
+        w1_bf = shared.tile([P, PACK, P, PACK], BF16, name="w1_bf", align_bytes=64, offset=8192)
+
+        def round_w1(i):
+            m0, m1 = PIECES[i]
+            share = SCALAR_SHARES[i]
+            src = w1_raw[i][:].rearrange("p j (m t) -> p m t j", t=PACK)
+            dst = w1_bf[:].rearrange("p t m j -> p m t j")[:, m0:m1]
+            if share > 0:
+                nc.scalar.copy(out=dst[:, :share], in_=src[:, :share])
+            if share < m1 - m0:
+                nc.vector.tensor_copy(out=dst[:, share:], in_=src[:, share:])
+
+        round_w1(0)
+        round_w1(1)
         xs_picked = keep.tile([P, S], U8, name="xs_picked", align_bytes=64)
         nc.vector.tensor_copy(xs_picked[:], xs_table[:].indirect(offsets[:]))
-        nc.vector.tensor_copy(out=x_plane.bitcast(I32), in_=xs_picked[:].bitcast(I32))
-        for j in range(1, 4):
-            nc.scalar.dma_start(
-                out=both_planes[j:P:QUAD, :].bitcast(I32),
-                in_=both_planes[8 * j : P : QUAD, :].bitcast(I32),
+        round_w1(2)
+        round_w1(3)
+        nc.vector.tensor_copy(out=x_plane[:].bitcast(I32), in_=xs_picked[:].bitcast(I32))
+
+        def place_rows(plane):
+            for j in range(1, 4):
+                nc.sync.dma_start(out=plane[j:P:QUAD, :].bitcast(I32), in_=plane[8 * j : P : QUAD, :].bitcast(I32))
+
+        place_rows(x_plane)
+        w2w_raw = shared.tile([P, H], I32, name="w2w_raw", align_bytes=64, offset=0)
+        nc.sync.dma_start(out=w2w_raw[:], in_=w2_words[0].rearrange("p n t -> p (n t)").bitcast(I32))
+
+        w1_codes = keep.tile([P, H], U32, name="w1_codes", align_bytes=64)
+        w1_plane = keep.tile([P, H], U8, name="w1_plane", align_bytes=64)
+        for t in range(PACK):
+            nc.vector.quantize_mx(
+                out=w1_codes[:, t * P : (t + 1) * P].bitcast(FP8X4),
+                scales=w1_plane[:, t * P : (t + 1) * P],
+                in_=w1_bf[:, t].rearrange("p m j -> p (m j)"),
             )
+
+        w2_plane = shared.tile([P, H], U8, name="w2_plane", align_bytes=64, offset=8192)
+        nc.vector.tensor_copy(
+            out=w2_plane[:].rearrange("p (t m) -> p t m", t=PACK),
+            in_=w2s_raw[:].rearrange("p (m t) -> p t m", t=PACK),
+        )
+        place_rows(w2_plane)
 
         x_codes = keep.tile([P, S], U32, name="x_codes", align_bytes=64)
         for g in range(S // GATHER):
@@ -76,44 +116,10 @@ def tile_picked_phmlp_relu_po_kernel(tc, x_words, x_scales, w1, w2_words, w2_sca
                 xw_table[:].indirect(offsets[:, g * GATHER // 16 : (g + 1) * GATHER // 16]),
             )
 
-        w2w_raw = keep.tile([P, 4 * H], U8, name="w2w_raw")
-        nc.sync.dma_start(out=w2w_raw[:].bitcast(I32), in_=w2_words[0].rearrange("p n t -> p (n t)").bitcast(I32))
-
-        w1_codes = keep.tile([P, H], U32, name="w1_codes", align_bytes=64)
-        w1_plane = keep.tile([P, H], U8, name="w1_plane", align_bytes=64)
-        w1_bf = [shared.tile([P, PACK, HALF, PACK], BF16, name="w1_bf%d" % half, align_bytes=64, offset=4096 * half) for half in range(2)]
-
-        def round_w1(i, on_scalar, tiles_a_copy):
-            m0, m1 = PIECES[i]
-            src = w1_raw[i][:].rearrange("p j (m t) -> p m t j", t=PACK)
-            dst = w1_bf[m0 // HALF][:].rearrange("p t m j -> p m t j")[:, m0 % HALF : m0 % HALF + m1 - m0]
-            nc.scalar.copy(out=dst[:, :on_scalar], in_=src[:, :on_scalar])
-            for t0 in range(0, PACK, tiles_a_copy):
-                nc.vector.tensor_copy(out=dst[:, on_scalar:, t0 : t0 + tiles_a_copy], in_=src[:, on_scalar:, t0 : t0 + tiles_a_copy])
-
-        def quantise_w1(half):
-            for t in range(PACK):
-                c0 = t * P + half * HALF
-                nc.vector.quantize_mx(
-                    out=w1_codes[:, c0 : c0 + HALF].bitcast(FP8X4),
-                    scales=w1_plane[:, c0 : c0 + HALF],
-                    in_=w1_bf[half][:, t].rearrange("p m j -> p (m j)"),
-                )
-
-        round_w1(0, 24, 4)
-        quantise_w1(0)
-        round_w1(1, 24, 4)
-        round_w1(2, 8, 2)
-        quantise_w1(1)
-        w2_plane = shared.tile([P, H], U8, name="w2_plane", align_bytes=64, offset=4096)
-        nc.vector.tensor_copy(
-            out=w2_plane[:].rearrange("p (t m) -> p t m", t=PACK),
-            in_=w2s_raw.rearrange("p (m t) -> p t m", t=PACK),
-        )
-        w2_codes = shared.tile([P, H], I32, name="w2_codes", align_bytes=64, offset=4096 + H)
+        w2_codes = keep.tile([P, H], I32, name="w2_codes", align_bytes=64)
         nc.vector.tensor_copy(
             out=w2_codes[:].rearrange("p (t m) -> p m t", t=PACK),
-            in_=w2w_raw[:].bitcast(I32).rearrange("p (m t) -> p m t", t=PACK),
+            in_=w2w_raw[:].rearrange("p (m t) -> p m t", t=PACK),
         )
 
         h_codes = keep.tile([P, S], U32, name="h_codes", align_bytes=64)
@@ -121,23 +127,22 @@ def tile_picked_phmlp_relu_po_kernel(tc, x_words, x_scales, w1, w2_words, w2_sca
         y_codes = keep.tile([P, S], U32, name="y_codes", align_bytes=64)
         y_plane = keep.tile([P, S], U8, name="y_plane", align_bytes=64)
         banks = [psum.tile([P, BANK], F32, name="bank%d" % i) for i in range(8)]
-        h_bf = {}
-        y_f32 = [keep.tile([P, PACK, w], F32, name="y_f32%d" % b) for b, w in enumerate(WIDTHS)]
-        y_bf = [keep.tile([P, w, PACK], BF16, name="y_bf%d" % b, align_bytes=64) for b, w in enumerate(WIDTHS)]
+        h_bf = [shared.tile([P, GROUP, PACK], BF16, name="h_bf%d" % b, align_bytes=64, offset=2048 * ((b - 1) % GROUPS)) for b in range(GROUPS)]
+        y_f32 = [keep.tile([P, PACK, GROUP], F32, name="y_f32%d" % b) for b in range(GROUPS)]
+        y_bf = [keep.tile([P, GROUP, PACK], BF16, name="y_bf%d" % b, align_bytes=64) for b in range(GROUPS)]
         out_rows = out_0.rearrange("(p t) n -> p t n", t=PACK)
         out_words = out_1[0].rearrange("p n t -> p (n t)").bitcast(I32)
 
-        def cols(b, last=None):
-            last = b if last is None else last
-            return slice(STARTS[b], STARTS[last] + WIDTHS[last])
+        def cols(b):
+            return slice(b * GROUP, (b + 1) * GROUP)
 
-        def view(bank, b):
-            return banks[bank][:, : PACK * WIDTHS[b]].rearrange("p (t n) -> p t n", t=PACK)
+        def view(bank):
+            return banks[bank][:].rearrange("p (t n) -> p t n", t=PACK)
 
-        def layer(bank, w_codes, w_plane, a_codes, a_plane, b, upper=None):
+        def layer(w_codes, w_plane, a_codes, a_plane, b, bank, upper):
             for t in range(PACK):
                 nc.tensor.matmul_mx(
-                    out=view(bank if upper is None or t < 2 else upper, b)[:, t, :],
+                    out=view(bank if t < 2 else upper)[:, t, :],
                     lhsT=w_codes[:, t * P : (t + 1) * P].bitcast(FP8X4),
                     lhsT_scale=w_plane[:, t * P : (t + 1) * P],
                     rhs=a_codes[:, cols(b)].bitcast(FP8X4),
@@ -146,24 +151,14 @@ def tile_picked_phmlp_relu_po_kernel(tc, x_words, x_scales, w1, w2_words, w2_sca
                     stop=True,
                 )
 
-        def first(b, bank):
-            layer(bank, w1_codes, w1_plane, x_codes, x_plane, b)
+        def first(b):
+            layer(w1_codes, w1_plane, x_codes, x_plane, b, b, b)
 
-        def second(b, bank):
-            layer(bank, w2_codes, w2_plane, h_codes, h_plane, b)
+        def second(b, bank, upper):
+            layer(w2_codes, w2_plane, h_codes, h_plane, b, bank, upper)
 
-        def second_split(b, bank, upper):
-            layer(bank, w2_codes, w2_plane, h_codes, h_plane, b, upper)
-
-        def result_split(b, bank, upper, vector_first):
-            early, late = (nc.vector.tensor_copy, nc.scalar.copy) if vector_first else (nc.scalar.copy, nc.vector.tensor_copy)
-            early(out=y_f32[b][:, :2], in_=view(bank, b)[:, :2])
-            late(out=y_f32[b][:, 2:], in_=view(upper, b)[:, 2:])
-            nc.sync.dma_start(out=out_rows[:, :, cols(b)], in_=y_f32[b][:])
-
-        def relu(b, bank, on_vector, tag):
-            h_bf[b] = keep.tile([P, WIDTHS[b], PACK], BF16, name="h_bf%d" % b, tag=tag, align_bytes=64)
-            stepped = view(bank, b).rearrange("p t n -> p n t")
+        def relu(b, on_vector):
+            stepped = view(b).rearrange("p t n -> p n t")
             if on_vector:
                 nc.vector.tensor_scalar(h_bf[b][:], stepped, 0.0, None, MAX)
             else:
@@ -176,12 +171,17 @@ def tile_picked_phmlp_relu_po_kernel(tc, x_words, x_scales, w1, w2_words, w2_sca
                 in_=src_bf[b][:].rearrange("p n t -> p (n t)"),
             )
 
-        def result(b, bank, on_vector, queue):
-            if on_vector:
-                nc.vector.tensor_copy(out=y_f32[b][:], in_=view(bank, b))
-            else:
-                nc.scalar.copy(out=y_f32[b][:], in_=view(bank, b))
-            queue.dma_start(out=out_rows[:, :, cols(b)], in_=y_f32[b][:])
+        def store_result(b):
+            nc.sync.dma_start(out=out_rows[:, :, cols(b)], in_=y_f32[b][:])
+
+        def result(b, bank):
+            nc.scalar.copy(out=y_f32[b][:], in_=view(bank))
+            store_result(b)
+
+        def result_split(b, bank, upper, early, late):
+            early(out=y_f32[b][:, :2], in_=view(bank)[:, :2])
+            late(out=y_f32[b][:, 2:], in_=view(upper)[:, 2:])
+            store_result(b)
 
         def rounded(b):
             nc.vector.tensor_copy(
@@ -189,51 +189,45 @@ def tile_picked_phmlp_relu_po_kernel(tc, x_words, x_scales, w1, w2_words, w2_sca
                 in_=y_f32[b][:].rearrange("p t (c i) -> p c t i", i=4),
             )
 
-        def rounded_from_bank(b, bank):
-            nc.scalar.copy(out=y_bf[b][:], in_=view(bank, b).rearrange("p t n -> p n t"))
-
-        def store_words(b, last):
-            nc.sync.dma_start(out=out_words[:, cols(b, last)], in_=y_codes[:, cols(b, last)].bitcast(I32))
-
-        for bank, rows, width in ((5, P, GATHER), (6, HALF, S), (7, HALF, S)):
+        for bank, c0, c1 in ((4, 0, P), (5, P, 2 * P), (6, 2 * P, 3 * P), (7, 0, H), (4, 0, H)):
             nc.tensor.matmul_mx(
-                out=banks[bank][:rows, :width],
-                lhsT=x_codes[:, :rows].bitcast(FP8X4),
-                lhsT_scale=xs_picked[:, :rows],
-                rhs=x_codes[:, :width].bitcast(FP8X4),
-                rhs_scale=xs_picked[:, :width],
+                out=banks[bank][:WARM_COLUMNS, : c1 - c0],
+                lhsT=w1_codes[:, :WARM_COLUMNS].bitcast(FP8X4),
+                lhsT_scale=w1_plane[:, :WARM_COLUMNS],
+                rhs=w1_codes[:, c0:c1].bitcast(FP8X4),
+                rhs_scale=w1_plane[:, c0:c1],
                 start=True,
                 stop=True,
             )
-        first(0, 0)
-        first(1, 1)
-        relu(0, 0, False, "h0")
-        first(2, 2)
-        first(3, 3)
-        relu(1, 1, True, "h1")
+        first(0)
+        first(1)
+        relu(0, False)
+        first(2)
+        first(3)
+        relu(1, True)
         quantise(h_codes, h_plane, h_bf, 0)
-        relu(2, 2, False, "h2")
-        second_split(0, 4, 0)
+        relu(2, False)
+        second(0, 4, 0)
         quantise(h_codes, h_plane, h_bf, 1)
-        second(1, 5)
-        relu(3, 3, False, "h3")
+        second(1, 5, 5)
+        relu(3, False)
         quantise(h_codes, h_plane, h_bf, 2)
-        second_split(2, 6, 1)
-        result_split(0, 4, 0, True)
+        second(2, 6, 1)
+        result_split(0, 4, 0, nc.vector.tensor_copy, nc.scalar.copy)
         quantise(h_codes, h_plane, h_bf, 3)
-        second(3, 7)
-        result(1, 5, False, nc.sync)
+        second(3, 7, 7)
+        result(1, 5)
         rounded(0)
-        result_split(2, 6, 1, False)
+        result_split(2, 6, 1, nc.scalar.copy, nc.vector.tensor_copy)
         rounded(1)
-        result(3, 7, False, nc.sync)
+        result(3, 7)
         rounded(2)
         quantise(y_codes, y_plane, y_bf, 0)
-        rounded_from_bank(3, 7)
+        nc.scalar.copy(out=y_bf[3][:], in_=view(7).rearrange("p t n -> p n t"))
         quantise(y_codes, y_plane, y_bf, 1)
         quantise(y_codes, y_plane, y_bf, 2)
         quantise(y_codes, y_plane, y_bf, 3)
-        store_words(0, 3)
+        nc.sync.dma_start(out=out_words, in_=y_codes[:].bitcast(I32))
         for q in range(4):
             nc.scalar.dma_start(
                 out=out_2[0, 4 * q : 4 * q + 4, :].bitcast(I32),

@@ -22,8 +22,7 @@ GROUP = 128
 GROUPS = S // GROUP
 BANK = 512
 GATHER = 256
-PIECES = ((0, 32), (32, 64), (64, 96), (96, 128))
-SCALAR_SHARES = (0, 32, 32, 10)
+SCALAR_SHARES = (96, 40)
 WARM_COLUMNS = 32
 
 
@@ -46,50 +45,39 @@ def tile_picked_phmlp_relu_po_kernel(tc, x_words, x_scales, w1, w2_words, w2_sca
         nc.scalar.dma_start(out=w2s_raw[0:P:8, :].bitcast(I32), in_=w2_scales[0].bitcast(I32))
 
         w1_rows = w1.rearrange("(p j) c -> p j c", j=PACK)
-        w1_raw = [
-            shared.tile([P, PACK, PACK * (m1 - m0)], F32, name="w1_raw%d" % i, align_bytes=64, offset=12288 + 16 * PACK * (P - m1))
-            for i, (m0, m1) in enumerate(PIECES)
-        ]
+        w1_raw = [shared.tile([P, 2, H], F32, name="w1_raw%d" % i, align_bytes=64, offset=12288 + 4096 * (1 - i)) for i in range(2)]
 
         def load_w1(i):
-            m0, m1 = PIECES[i]
-            nc.sync.dma_start(out=w1_raw[i][:], in_=w1_rows[:, :, PACK * m0 : PACK * m1])
+            nc.sync.dma_start(out=w1_raw[i][:], in_=w1_rows[:, 2 * i : 2 * i + 2, :])
 
         load_w1(0)
-        load_w1(1)
         offsets = keep.tile([P, S // 16], U16, name="offsets")
         nc.sync.dma_start(offsets[:], offs)
         nc.sync.dma_start(out=xs_table[0:P:8, :].bitcast(I32), in_=x_scales[0].bitcast(I32))
-        load_w1(2)
-        load_w1(3)
+        load_w1(1)
         xw_table = keep.tile([P, T], U32, name="xw_table")
         nc.sync.dma_start(out=xw_table[:].bitcast(I32), in_=x_words[0].rearrange("p n t -> p (n t)").bitcast(I32))
 
         w1_bf = shared.tile([P, PACK, P, PACK], BF16, name="w1_bf", align_bytes=64, offset=8192)
 
         def round_w1(i):
-            m0, m1 = PIECES[i]
             share = SCALAR_SHARES[i]
             src = w1_raw[i][:].rearrange("p j (m t) -> p m t j", t=PACK)
-            dst = w1_bf[:].rearrange("p t m j -> p m t j")[:, m0:m1]
-            if share > 0:
-                nc.scalar.copy(out=dst[:, :share], in_=src[:, :share])
-            if share < m1 - m0:
-                nc.vector.tensor_copy(out=dst[:, share:], in_=src[:, share:])
+            dst = w1_bf[:].rearrange("p t m j -> p m t j")[:, :, :, 2 * i : 2 * i + 2]
+            nc.scalar.copy(out=dst[:, :share], in_=src[:, :share])
+            nc.vector.tensor_copy(out=dst[:, share:], in_=src[:, share:])
 
         round_w1(0)
-        round_w1(1)
         xs_picked = keep.tile([P, S], U8, name="xs_picked", align_bytes=64)
         nc.vector.tensor_copy(xs_picked[:], xs_table[:].indirect(offsets[:]))
-        round_w1(2)
-        round_w1(3)
+        round_w1(1)
         nc.vector.tensor_copy(out=x_plane[:].bitcast(I32), in_=xs_picked[:].bitcast(I32))
 
-        def place_rows(plane):
+        def place_rows(queue, plane):
             for j in range(1, 4):
-                nc.sync.dma_start(out=plane[j:P:QUAD, :].bitcast(I32), in_=plane[8 * j : P : QUAD, :].bitcast(I32))
+                queue.dma_start(out=plane[j:P:QUAD, :].bitcast(I32), in_=plane[8 * j : P : QUAD, :].bitcast(I32))
 
-        place_rows(x_plane)
+        place_rows(nc.scalar, x_plane)
         w2w_raw = shared.tile([P, H], I32, name="w2w_raw", align_bytes=64, offset=0)
         nc.sync.dma_start(out=w2w_raw[:], in_=w2_words[0].rearrange("p n t -> p (n t)").bitcast(I32))
 
@@ -107,7 +95,7 @@ def tile_picked_phmlp_relu_po_kernel(tc, x_words, x_scales, w1, w2_words, w2_sca
             out=w2_plane[:].rearrange("p (t m) -> p t m", t=PACK),
             in_=w2s_raw[:].rearrange("p (m t) -> p t m", t=PACK),
         )
-        place_rows(w2_plane)
+        place_rows(nc.sync, w2_plane)
 
         x_codes = keep.tile([P, S], U32, name="x_codes", align_bytes=64)
         for g in range(S // GATHER):

@@ -22,7 +22,9 @@ GROUP = 128
 GROUPS = S // GROUP
 BANK = 512
 GATHER = 256
-SCALAR_SHARES = (96, 40)
+SCALAR_SHARES = (56, 20)
+HALF = H // 2
+LINE = 256
 WARM_COLUMNS = 32
 
 
@@ -37,52 +39,53 @@ def tile_picked_phmlp_relu_po_kernel(tc, x_words, x_scales, w1, w2_words, w2_sca
         nc.gpsimd.memset(warm[:, 0:1], 0.0)
         nc.scalar.activation(warm[:, 1:2], warm[:, 0:1], RELU)
 
-        x_plane = shared.tile([P, S], U8, name="x_plane", align_bytes=64, offset=12288)
-        w2s_raw = keep.tile([P, H], U8, name="w2s_raw")
-        xs_table = keep.tile([P, T], U8, name="xs_table")
+        w2s_raw = keep.tile([P, H], U8, name="w2s_raw", align_bytes=LINE)
+        xs_table = keep.tile([P, T], U8, name="xs_table", align_bytes=LINE)
         nc.vector.memset(xs_table[:].bitcast(I32), 0)
         nc.vector.memset(w2s_raw[:].bitcast(I32), 0)
+        x_plane = keep.tile([P, S], U8, name="x_plane", align_bytes=LINE)
+        nc.vector.memset(x_plane[:].bitcast(I32), 0)
         nc.scalar.dma_start(out=w2s_raw[0:P:8, :].bitcast(I32), in_=w2_scales[0].bitcast(I32))
 
         w1_rows = w1.rearrange("(p j) c -> p j c", j=PACK)
-        w1_raw = [shared.tile([P, 2, H], F32, name="w1_raw%d" % i, align_bytes=64, offset=12288 + 4096 * (1 - i)) for i in range(2)]
+        w1_raw = [shared.tile([P, PACK, HALF], F32, name="w1_raw%d" % i, align_bytes=LINE, offset=4096 * (1 - i)) for i in range(2)]
 
         def load_w1(i):
-            nc.sync.dma_start(out=w1_raw[i][:], in_=w1_rows[:, 2 * i : 2 * i + 2, :])
+            nc.sync.dma_start(out=w1_raw[i][:], in_=w1_rows[:, :, i * HALF : (i + 1) * HALF])
 
         load_w1(0)
         offsets = keep.tile([P, S // 16], U16, name="offsets")
         nc.sync.dma_start(offsets[:], offs)
         nc.sync.dma_start(out=xs_table[0:P:8, :].bitcast(I32), in_=x_scales[0].bitcast(I32))
         load_w1(1)
-        xw_table = keep.tile([P, T], U32, name="xw_table")
+        xw_table = keep.tile([P, T], U32, name="xw_table", align_bytes=LINE)
         nc.sync.dma_start(out=xw_table[:].bitcast(I32), in_=x_words[0].rearrange("p n t -> p (n t)").bitcast(I32))
 
-        w1_bf = shared.tile([P, PACK, P, PACK], BF16, name="w1_bf", align_bytes=64, offset=8192)
+        w1_bf = shared.tile([P, PACK, P, PACK], BF16, name="w1_bf", align_bytes=LINE, offset=8192)
 
-        def round_w1(i):
+        def round_w1(i, tiles):
             share = SCALAR_SHARES[i]
             src = w1_raw[i][:].rearrange("p j (m t) -> p m t j", t=PACK)
-            dst = w1_bf[:].rearrange("p t m j -> p m t j")[:, :, :, 2 * i : 2 * i + 2]
+            dst = w1_bf[:].rearrange("p t m j -> p m t j")[:, i * HALF // PACK : (i + 1) * HALF // PACK]
             nc.scalar.copy(out=dst[:, :share], in_=src[:, :share])
-            nc.vector.tensor_copy(out=dst[:, share:], in_=src[:, share:])
+            for t in range(0, PACK, tiles):
+                nc.vector.tensor_copy(out=dst[:, share:, t : t + tiles], in_=src[:, share:, t : t + tiles])
 
-        round_w1(0)
-        xs_picked = keep.tile([P, S], U8, name="xs_picked", align_bytes=64)
+        round_w1(0, PACK)
+        xs_picked = keep.tile([P, S], U8, name="xs_picked", align_bytes=LINE)
         nc.vector.tensor_copy(xs_picked[:], xs_table[:].indirect(offsets[:]))
-        round_w1(1)
-        nc.vector.tensor_copy(out=x_plane[:].bitcast(I32), in_=xs_picked[:].bitcast(I32))
 
-        def place_rows(queue, plane):
-            for j in range(1, 4):
-                queue.dma_start(out=plane[j:P:QUAD, :].bitcast(I32), in_=plane[8 * j : P : QUAD, :].bitcast(I32))
+        def place_rows(plane, spread, first_row):
+            for j in range(first_row, 4):
+                nc.sync.dma_start(out=plane[j:P:QUAD, :].bitcast(I32), in_=spread[8 * j : P : QUAD, :].bitcast(I32))
 
-        place_rows(nc.scalar, x_plane)
-        w2w_raw = shared.tile([P, H], I32, name="w2w_raw", align_bytes=64, offset=0)
+        place_rows(x_plane, xs_picked, 0)
+        round_w1(1, 2)
+        w2w_raw = shared.tile([P, H], I32, name="w2w_raw", align_bytes=LINE, offset=0)
         nc.sync.dma_start(out=w2w_raw[:], in_=w2_words[0].rearrange("p n t -> p (n t)").bitcast(I32))
 
-        w1_codes = keep.tile([P, H], U32, name="w1_codes", align_bytes=64)
-        w1_plane = keep.tile([P, H], U8, name="w1_plane", align_bytes=64)
+        w1_codes = keep.tile([P, H], U32, name="w1_codes", align_bytes=LINE)
+        w1_plane = keep.tile([P, H], U8, name="w1_plane", align_bytes=LINE)
         for t in range(PACK):
             nc.vector.quantize_mx(
                 out=w1_codes[:, t * P : (t + 1) * P].bitcast(FP8X4),
@@ -90,34 +93,34 @@ def tile_picked_phmlp_relu_po_kernel(tc, x_words, x_scales, w1, w2_words, w2_sca
                 in_=w1_bf[:, t].rearrange("p m j -> p (m j)"),
             )
 
-        w2_plane = shared.tile([P, H], U8, name="w2_plane", align_bytes=64, offset=8192)
+        w2_plane = shared.tile([P, H], U8, name="w2_plane", align_bytes=LINE, offset=8192)
         nc.vector.tensor_copy(
             out=w2_plane[:].rearrange("p (t m) -> p t m", t=PACK),
             in_=w2s_raw[:].rearrange("p (m t) -> p t m", t=PACK),
         )
-        place_rows(nc.sync, w2_plane)
+        place_rows(w2_plane, w2_plane, 1)
 
-        x_codes = keep.tile([P, S], U32, name="x_codes", align_bytes=64)
+        x_codes = keep.tile([P, S], U32, name="x_codes", align_bytes=LINE)
         for g in range(S // GATHER):
             nc.vector.tensor_copy(
                 x_codes[:, g * GATHER : (g + 1) * GATHER],
                 xw_table[:].indirect(offsets[:, g * GATHER // 16 : (g + 1) * GATHER // 16]),
             )
 
-        w2_codes = keep.tile([P, H], I32, name="w2_codes", align_bytes=64)
+        w2_codes = keep.tile([P, H], I32, name="w2_codes", align_bytes=LINE)
         nc.vector.tensor_copy(
             out=w2_codes[:].rearrange("p (t m) -> p m t", t=PACK),
             in_=w2w_raw[:].rearrange("p (m t) -> p m t", t=PACK),
         )
 
-        h_codes = keep.tile([P, S], U32, name="h_codes", align_bytes=64)
-        h_plane = keep.tile([P, S], U8, name="h_plane", align_bytes=64)
-        y_codes = keep.tile([P, S], U32, name="y_codes", align_bytes=64)
-        y_plane = keep.tile([P, S], U8, name="y_plane", align_bytes=64)
+        h_codes = keep.tile([P, S], U32, name="h_codes", align_bytes=LINE)
+        h_plane = keep.tile([P, S], U8, name="h_plane", align_bytes=LINE)
+        y_codes = keep.tile([P, S], U32, name="y_codes", align_bytes=LINE)
+        y_plane = keep.tile([P, S], U8, name="y_plane", align_bytes=LINE)
         banks = [psum.tile([P, BANK], F32, name="bank%d" % i) for i in range(8)]
-        h_bf = [shared.tile([P, GROUP, PACK], BF16, name="h_bf%d" % b, align_bytes=64, offset=2048 * ((b - 1) % GROUPS)) for b in range(GROUPS)]
-        y_f32 = [keep.tile([P, PACK, GROUP], F32, name="y_f32%d" % b) for b in range(GROUPS)]
-        y_bf = [keep.tile([P, GROUP, PACK], BF16, name="y_bf%d" % b, align_bytes=64) for b in range(GROUPS)]
+        h_bf = [shared.tile([P, GROUP, PACK], BF16, name="h_bf%d" % b, align_bytes=LINE, offset=2048 * ((b - 1) % GROUPS)) for b in range(GROUPS)]
+        y_f32 = [keep.tile([P, PACK, GROUP], F32, name="y_f32%d" % b, align_bytes=LINE) for b in range(GROUPS)]
+        y_bf = [keep.tile([P, GROUP, PACK], BF16, name="y_bf%d" % b, align_bytes=LINE) for b in range(GROUPS)]
         out_rows = out_0.rearrange("(p t) n -> p t n", t=PACK)
         out_words = out_1[0].rearrange("p n t -> p (n t)").bitcast(I32)
 
@@ -177,7 +180,7 @@ def tile_picked_phmlp_relu_po_kernel(tc, x_words, x_scales, w1, w2_words, w2_sca
                 in_=y_f32[b][:].rearrange("p t (c i) -> p c t i", i=4),
             )
 
-        for bank, c0, c1 in ((4, 0, P), (5, P, 2 * P), (6, 2 * P, 3 * P), (7, 0, H), (4, 0, H)):
+        for bank, c0, c1 in ((4, 0, P), (5, 0, P), (6, P, 2 * P), (7, 2 * P, 3 * P), (4, 0, H), (5, 0, H)):
             nc.tensor.matmul_mx(
                 out=banks[bank][:WARM_COLUMNS, : c1 - c0],
                 lhsT=w1_codes[:, :WARM_COLUMNS].bitcast(FP8X4),

from contextlib import ExitStack

import concourse.mybir as mybir

K, T, S, H = 512, 2048, 512, 512
FLOPS = 2 * K * H * S + 2 * H * H * S

F32 = mybir.dt.float32
BF16 = mybir.dt.bfloat16
I32 = mybir.dt.int32
U32 = mybir.dt.uint32
U16 = mybir.dt.uint16
U8 = mybir.dt.uint8
FP8X4 = mybir.dt.float8_e4m3fn_x4
RELU = mybir.ActivationFunctionType.Relu
MAX = mybir.AluOpType.max

P = 128
PACK = 4
QUAD = 32
GROUP = 128
GROUPS = S // GROUP
BANK = 512
GATHER = 256
SCALAR_SHARES = (56, 20)
HALF = H // 2
LINE = 256
WARM_COLUMNS = 32


def tile_picked_phmlp_relu_po_kernel(tc, x_words, x_scales, w1, w2_words, w2_scales, offs, out_0, out_1, out_2):
    nc = tc.nc
    with ExitStack() as ctx:
        keep = ctx.enter_context(tc.tile_pool(name="keep", bufs=1))
        shared = ctx.enter_context(tc.tile_pool(name="shared", bufs=1))
        psum = ctx.enter_context(tc.psum_pool(name="psum", bufs=1))

        warm = keep.tile([P, 2], F32, name="warm")
        nc.gpsimd.memset(warm[:, 0:1], 0.0)
        nc.scalar.activation(warm[:, 1:2], warm[:, 0:1], RELU)

        w2s_raw = keep.tile([P, H], U8, name="w2s_raw", align_bytes=LINE)
        xs_table = keep.tile([P, T], U8, name="xs_table", align_bytes=LINE)
        nc.vector.memset(xs_table[:].bitcast(I32), 0)
        nc.vector.memset(w2s_raw[:].bitcast(I32), 0)
        x_plane = keep.tile([P, S], U8, name="x_plane", align_bytes=LINE)
        nc.vector.memset(x_plane[:].bitcast(I32), 0)
        nc.scalar.dma_start(out=w2s_raw[0:P:8, :].bitcast(I32), in_=w2_scales[0].bitcast(I32))

        w1_rows = w1.rearrange("(p j) c -> p j c", j=PACK)
        w1_raw = [shared.tile([P, PACK, HALF], F32, name="w1_raw%d" % i, align_bytes=LINE, offset=4096 * (1 - i)) for i in range(2)]

        def load_w1(i):
            nc.sync.dma_start(out=w1_raw[i][:], in_=w1_rows[:, :, i * HALF : (i + 1) * HALF])

        load_w1(0)
        offsets = keep.tile([P, S // 16], U16, name="offsets")
        nc.sync.dma_start(offsets[:], offs)
        nc.sync.dma_start(out=xs_table[0:P:8, :].bitcast(I32), in_=x_scales[0].bitcast(I32))
        load_w1(1)
        xw_table = keep.tile([P, T], U32, name="xw_table", align_bytes=LINE)
        nc.sync.dma_start(out=xw_table[:].bitcast(I32), in_=x_words[0].rearrange("p n t -> p (n t)").bitcast(I32))

        w1_bf = shared.tile([P, PACK, P, PACK], BF16, name="w1_bf", align_bytes=LINE, offset=8192)

        def round_w1(i, tiles):
            share = SCALAR_SHARES[i]
            src = w1_raw[i][:].rearrange("p j (m t) -> p m t j", t=PACK)
            dst = w1_bf[:].rearrange("p t m j -> p m t j")[:, i * HALF // PACK : (i + 1) * HALF // PACK]
            nc.scalar.copy(out=dst[:, :share], in_=src[:, :share])
            for t in range(0, PACK, tiles):
                nc.vector.tensor_copy(out=dst[:, share:, t : t + tiles], in_=src[:, share:, t : t + tiles])

        round_w1(0, PACK)
        xs_picked = keep.tile([P, S], U8, name="xs_picked", align_bytes=LINE)
        nc.vector.tensor_copy(xs_picked[:], xs_table[:].indirect(offsets[:]))

        def place_rows(plane, spread, first_row):
            for j in range(first_row, 4):
                nc.sync.dma_start(out=plane[j:P:QUAD, :].bitcast(I32), in_=spread[8 * j : P : QUAD, :].bitcast(I32))

        place_rows(x_plane, xs_picked, 0)
        round_w1(1, 2)
        w2w_raw = shared.tile([P, H], I32, name="w2w_raw", align_bytes=LINE, offset=0)
        nc.sync.dma_start(out=w2w_raw[:], in_=w2_words[0].rearrange("p n t -> p (n t)").bitcast(I32))

        w1_codes = keep.tile([P, H], U32, name="w1_codes", align_bytes=LINE)
        w1_plane = keep.tile([P, H], U8, name="w1_plane", align_bytes=LINE)
        for t in range(PACK):
            nc.vector.quantize_mx(
                out=w1_codes[:, t * P : (t + 1) * P].bitcast(FP8X4),
                scales=w1_plane[:, t * P : (t + 1) * P],
                in_=w1_bf[:, t].rearrange("p m j -> p (m j)"),
            )

        w2_plane = shared.tile([P, H], U8, name="w2_plane", align_bytes=LINE, offset=8192)
        nc.vector.tensor_copy(
            out=w2_plane[:].rearrange("p (t m) -> p t m", t=PACK),
            in_=w2s_raw[:].rearrange("p (m t) -> p t m", t=PACK),
        )
        place_rows(w2_plane, w2_plane, 1)

        x_codes = keep.tile([P, S], U32, name="x_codes", align_bytes=LINE)
        for g in range(S // GATHER):
            nc.vector.tensor_copy(
                x_codes[:, g * GATHER : (g + 1) * GATHER],
                xw_table[:].indirect(offsets[:, g * GATHER // 16 : (g + 1) * GATHER // 16]),
            )

        w2_codes = keep.tile([P, H], I32, name="w2_codes", align_bytes=LINE)
        nc.vector.tensor_copy(
            out=w2_codes[:].rearrange("p (t m) -> p m t", t=PACK),
            in_=w2w_raw[:].rearrange("p (m t) -> p m t", t=PACK),
        )

        h_codes = keep.tile([P, S], U32, name="h_codes", align_bytes=LINE)
        h_plane = keep.tile([P, S], U8, name="h_plane", align_bytes=LINE)
        y_codes = keep.tile([P, S], U32, name="y_codes", align_bytes=LINE)
        y_plane = keep.tile([P, S], U8, name="y_plane", align_bytes=LINE)
        banks = [psum.tile([P, BANK], F32, name="bank%d" % i) for i in range(8)]
        h_bf = [shared.tile([P, GROUP, PACK], BF16, name="h_bf%d" % b, align_bytes=LINE, offset=2048 * ((b - 1) % GROUPS)) for b in range(GROUPS)]
        y_f32 = [keep.tile([P, PACK, GROUP], F32, name="y_f32%d" % b, align_bytes=LINE) for b in range(GROUPS)]
        y_bf = [keep.tile([P, GROUP, PACK], BF16, name="y_bf%d" % b, align_bytes=LINE) for b in range(GROUPS)]
        out_rows = out_0.rearrange("(p t) n -> p t n", t=PACK)
        out_words = out_1[0].rearrange("p n t -> p (n t)").bitcast(I32)

        def cols(b):
            return slice(b * GROUP, (b + 1) * GROUP)

        def view(bank):
            return banks[bank][:].rearrange("p (t n) -> p t n", t=PACK)

        def layer(w_codes, w_plane, a_codes, a_plane, b, bank, upper):
            for t in range(PACK):
                nc.tensor.matmul_mx(
                    out=view(bank if t < 2 else upper)[:, t, :],
                    lhsT=w_codes[:, t * P : (t + 1) * P].bitcast(FP8X4),
                    lhsT_scale=w_plane[:, t * P : (t + 1) * P],
                    rhs=a_codes[:, cols(b)].bitcast(FP8X4),
                    rhs_scale=a_plane[:, cols(b)],
                    start=True,
                    stop=True,
                )

        def first(b):
            layer(w1_codes, w1_plane, x_codes, x_plane, b, b, b)

        def second(b, bank, upper):
            layer(w2_codes, w2_plane, h_codes, h_plane, b, bank, upper)

        def relu(b, on_vector):
            stepped = view(b).rearrange("p t n -> p n t")
            if on_vector:
                nc.vector.tensor_scalar(h_bf[b][:], stepped, 0.0, None, MAX)
            else:
                nc.scalar.activation(h_bf[b][:], stepped, RELU)

        def quantise(codes, plane, src_bf, b):
            nc.vector.quantize_mx(
                out=codes[:, cols(b)].bitcast(FP8X4),
                scales=plane[:, cols(b)],
                in_=src_bf[b][:].rearrange("p n t -> p (n t)"),
            )

        def store_result(b):
            nc.sync.dma_start(out=out_rows[:, :, cols(b)], in_=y_f32[b][:])

        def result(b, bank):
            nc.scalar.copy(out=y_f32[b][:], in_=view(bank))
            store_result(b)

        def result_split(b, bank, upper, early, late):
            early(out=y_f32[b][:, :2], in_=view(bank)[:, :2])
            late(out=y_f32[b][:, 2:], in_=view(upper)[:, 2:])
            store_result(b)

        def rounded(b):
            nc.vector.tensor_copy(
                out=y_bf[b][:].rearrange("p (c i) t -> p c t i", i=4),
                in_=y_f32[b][:].rearrange("p t (c i) -> p c t i", i=4),
            )

        for bank, c0, c1 in ((4, 0, P), (5, 0, P), (6, P, 2 * P), (7, 2 * P, 3 * P), (4, 0, H), (5, 0, H)):
            nc.tensor.matmul_mx(
                out=banks[bank][:WARM_COLUMNS, : c1 - c0],
                lhsT=w1_codes[:, :WARM_COLUMNS].bitcast(FP8X4),
                lhsT_scale=w1_plane[:, :WARM_COLUMNS],
                rhs=w1_codes[:, c0:c1].bitcast(FP8X4),
                rhs_scale=w1_plane[:, c0:c1],
                start=True,
                stop=True,
            )
        first(0)
        first(1)
        relu(0, False)
        first(2)
        first(3)
        relu(1, True)
        quantise(h_codes, h_plane, h_bf, 0)
        relu(2, False)
        second(0, 4, 0)
        quantise(h_codes, h_plane, h_bf, 1)
        second(1, 5, 5)
        relu(3, False)
        quantise(h_codes, h_plane, h_bf, 2)
        second(2, 6, 1)
        result_split(0, 4, 0, nc.vector.tensor_copy, nc.scalar.copy)
        quantise(h_codes, h_plane, h_bf, 3)
        second(3, 7, 7)
        result(1, 5)
        rounded(0)
        result_split(2, 6, 1, nc.scalar.copy, nc.vector.tensor_copy)
        rounded(1)
        result(3, 7)
        rounded(2)
        quantise(y_codes, y_plane, y_bf, 0)
        nc.scalar.copy(out=y_bf[3][:], in_=view(7).rearrange("p t n -> p n t"))
        quantise(y_codes, y_plane, y_bf, 1)
        quantise(y_codes, y_plane, y_bf, 2)
        quantise(y_codes, y_plane, y_bf, 3)
        nc.sync.dma_start(out=out_words, in_=y_codes[:].bitcast(I32))
        for q in range(4):
            nc.scalar.dma_start(
                out=out_2[0, 4 * q : 4 * q + 4, :].bitcast(I32),
                in_=y_plane[QUAD * q : QUAD * q + 4, :].bitcast(I32),
            )
